import numpy as np
import ml_dtypes


def mxq(x, axis, fmt="e4m3"):
    dtype, down = {"e4m3": (ml_dtypes.float8_e4m3fn, 7), "e5m2": (ml_dtypes.float8_e5m2, 14)}[fmt]
    v = np.moveaxis(np.asarray(x, np.float32).astype(ml_dtypes.bfloat16).astype(np.float64), axis, -1)
    blocks = v.reshape(v.shape[:-1] + (-1, 32))
    amax = np.abs(blocks).max(-1, keepdims=True)
    byte = np.maximum(np.where(amax > 0, np.frexp(amax)[1] - 1 + 127, 0) - down, 1)
    scale = np.exp2(byte - 127.0)
    codes = (blocks / scale).astype(np.float32).astype(dtype).astype(np.float64)
    return np.moveaxis((codes * scale).reshape(v.shape), -1, axis)


WIDE = False


def mx_kscale(k):
    if not WIDE:
        return np.ones(k)
    levels = np.array([10, -10, 5, -5, 0])
    if k % 512:
        return np.exp2(np.random.permutation(np.resize(levels, k // 32))).repeat(32)
    a = np.empty((k // 512, 16))
    for p in range(k // 512):
        a[p, :8] = np.random.permutation(np.resize(levels, 8))
        for g in range(8):
            far = levels[np.abs(levels - a[p, g]) >= 10]
            a[p, g + 8] = far[np.random.randint(len(far))]
    return np.exp2(a.ravel()).repeat(32)


def f64(x):
    return np.asarray(x).astype(np.float64)


def striped(idx):
    return np.tile(idx.reshape(-1, 16).T, (8, 1)).astype(np.uint16)


def unstriped(offs):
    return offs[:16].T.reshape(-1).astype(np.int64)


def pack_weight(w):
    k, n = w.shape
    w = f64(np.asarray(w, np.float32).astype(ml_dtypes.bfloat16)).reshape(k // 32, 32, n)
    amax = np.abs(w).max(1)
    byte = np.clip(np.where(amax > 0, np.frexp(amax)[1] - 1 + 127 - 7, 1), 1, 254)
    scaled = (w * np.exp2(127.0 - byte)[:, None, :]).reshape(k, n).astype(np.float32)
    words = np.ascontiguousarray(scaled.reshape(k // 512, 128, 4, n).transpose(0, 1, 3, 2)).astype(ml_dtypes.float8_e4m3fn).view(np.uint8)
    return words, np.ascontiguousarray(byte.astype(np.uint8).reshape(k // 512, 16, n))


def unpack_weight(words, scales):
    g, p, n, _ = words.shape
    vals = np.ascontiguousarray(words).view(ml_dtypes.float8_e4m3fn).astype(np.float64) * np.repeat(np.exp2(scales.astype(np.float64) - 127.0), 8, axis=1)[..., None]
    return vals.transpose(0, 1, 3, 2).reshape(g * 512, n)


def planes(y):
    n, m = y.shape
    v = y.astype(np.float32).astype(ml_dtypes.bfloat16).astype(np.float64).reshape(n // 32, 32, m)
    top = np.abs(v).max(1)
    byte = np.clip(np.where(top > 0, np.frexp(top)[1] - 1 + 127 - 7, 1), 1, 254)
    codes = (v * np.exp2(127.0 - byte)[:, None, :]).reshape(n, m).astype(np.float32).astype(ml_dtypes.float8_e4m3fn).view(np.uint8)
    words = codes.reshape(n // 512, 128, 4, m).transpose(0, 1, 3, 2)
    return np.ascontiguousarray(words), np.ascontiguousarray(byte.astype(np.uint8).reshape(n // 512, 16, m))


def sigmoid(v):
    return 1.0 / (1.0 + np.exp(-np.maximum(v, -700.0)))


K, T, S, H, U, J = 512, 1024, 512, 512, 1024, 512


def setup_inputs():
    n = np.random.standard_normal
    s = mx_kscale(K)[:, None]
    u = mx_kscale(H)
    packed_xT = pack_weight(n((K, T)) * s)
    return {
        "x_words": packed_xT[0],
        "x_scales": packed_xT[1],
        "mem": (n((H, U)) * u[:, None]).astype(np.float32),
        "w1": (n((K, H)) / np.sqrt(2 * K) / s).astype(np.float32),
        "w2": (n((K, H)) / np.sqrt(2 * K) / s).astype(np.float32),
        "r1": (n((H, J)) / np.sqrt(2 * H) / u[:, None]).astype(np.float32),
        "r2": (n((H, J)) / np.sqrt(2 * H) / u[:, None]).astype(np.float32),
        "unit": (np.random.uniform(0.6, 1.4, (H, 1)) / u[:, None]).astype(np.float32),
        "offs": striped(np.random.permutation(T)[:S]),
        "slot": striped(np.random.permutation(U)[:S]),
    }


def reference(x_words, x_scales, mem, w1, w2, r1, r2, unit, offs, slot):
    old = f64(mem)[:, unstriped(slot)]
    ov = f64(unit) * old
    xq = unpack_weight(x_words, x_scales)[:, unstriped(offs)]
    oldq = mxq(old, 0, "e4m3")
    z = sigmoid(mxq(f64(w1), 0, "e4m3").T @ xq + mxq(f64(r1), 0, "e4m3").T @ oldq)
    gg = np.tanh(mxq(f64(w2), 0, "e4m3").T @ xq + mxq(f64(r2), 0, "e4m3").T @ oldq)
    out_0 = ov + z * (gg - ov)
    return (out_0,) + planes(out_0)

@@ -1,0 +1,241 @@
+from contextlib import ExitStack
+
+import concourse.mybir as mybir
+
+K, T, S, H, U = 512, 1024, 512, 512, 1024
+FLOPS = 4 * 2 * K * H * S
+
+F32 = mybir.dt.float32
+BF16 = mybir.dt.bfloat16
+I32 = mybir.dt.int32
+U32 = mybir.dt.uint32
+U16 = mybir.dt.uint16
+U8 = mybir.dt.uint8
+FP8X4 = mybir.dt.float8_e4m3fn_x4
+TANH = mybir.ActivationFunctionType.Tanh
+MULT = mybir.AluOpType.mult
+ADD = mybir.AluOpType.add
+SUB = mybir.AluOpType.subtract
+
+P = 128
+PACK = 4
+HALF = 256
+
+
+def tile_picked_ytgn_gru_po_kernel(
+    tc, x_words, x_scales, mem, w1, w2, r1, r2, unit, offs, slot, out_0, out_1, out_2
+):
+    nc = tc.nc
+    with ExitStack() as ctx:
+        sb = ctx.enter_context(tc.tile_pool(name="sb", bufs=1))
+        psum = ctx.enter_context(tc.psum_pool(name="psum", bufs=1))
+
+        def copy_on(engine, out, in_):
+            if engine == "scalar":
+                nc.scalar.copy(out=out, in_=in_)
+            else:
+                nc.vector.tensor_copy(out=out, in_=in_)
+
+        slot_t = sb.tile([P, S // 16], U16, name="slot_t")
+        offs_t = sb.tile([P, S // 16], U16, name="offs_t")
+        nc.sync.dma_start(slot_t[:], slot)
+        nc.sync.dma_start(offs_t[:], offs)
+
+        xs_all = sb.tile([P, T], U8, name="xs_all", align_bytes=64)
+        nc.vector.memset(xs_all[:].bitcast(I32), 0)
+        for q in range(4):
+            nc.scalar.dma_start(
+                xs_all[32 * q : 32 * q + 4, :].bitcast(I32), x_scales[0, 4 * q : 4 * q + 4, :].bitcast(I32)
+            )
+        unit_t = sb.tile([P, PACK], F32, name="unit_t")
+        nc.scalar.dma_start(unit_t[:], unit.rearrange("(p t) o -> p (t o)", t=PACK))
+
+        zero_in = sb.tile([P, 1], F32, name="zero_in")
+        zero = sb.tile([P, 1], F32, name="zero")
+        nc.vector.memset(zero_in[:], 0.0)
+        nc.scalar.activation(out=zero[:], in_=zero_in[:], func=TANH)
+
+        mem_rows = mem.rearrange("(p t) c -> p t c", t=PACK)
+        mem_t = [sb.tile([P, U], F32, name=f"mem{t}") for t in range(PACK)]
+        weights = {"w1": w1, "w2": w2, "r1": r1, "r2": r2}
+        raw = {
+            (n, h): sb.tile([P, PACK, HALF], F32, name=f"raw_{n}_{h}") for n in weights for h in range(2)
+        }
+        xw_all = sb.tile([P, T], I32, name="xw_all", align_bytes=64)
+
+        def load_mem(t):
+            nc.sync.dma_start(mem_t[t][:], mem_rows[:, t, :])
+
+        def load_weight(n, h):
+            rows = weights[n].rearrange("(p j) c -> p j c", j=PACK)
+            nc.sync.dma_start(raw[n, h][:], rows[:, :, h * HALF : (h + 1) * HALF])
+
+        load_mem(0)
+        load_mem(1)
+        load_weight("r2", 0)
+        load_mem(2)
+        load_mem(3)
+        load_weight("r2", 1)
+        nc.sync.dma_start(xw_all[:], x_words[0].rearrange("p n t -> p (n t)").bitcast(I32))
+        for n in ("w2", "w1", "r1"):
+            load_weight(n, 0)
+            load_weight(n, 1)
+
+        old = sb.tile([P, PACK, S], F32, name="old")
+        old_bf = sb.tile([P, S, PACK], BF16, name="old_bf", align_bytes=64)
+        old_codes = sb.tile([P, S], U32, name="old_codes", align_bytes=64)
+        old_scales = sb.tile([P, S], U8, name="old_scales", align_bytes=64)
+        x_codes = sb.tile([P, S], U32, name="x_codes", align_bytes=64)
+        x_sc = sb.tile([P, S], U8, name="x_sc", align_bytes=64)
+        w_bf = {n: sb.tile([P, PACK, P, PACK], BF16, name=f"bf_{n}", align_bytes=64) for n in weights}
+        w_codes = {n: sb.tile([P, H], U32, name=f"codes_{n}", align_bytes=64) for n in weights}
+        w_scales = {n: sb.tile([P, H], U8, name=f"scales_{n}", align_bytes=64) for n in weights}
+
+        def gather_mem(t):
+            nc.vector.tensor_copy(old[:, t, :], mem_t[t][:].indirect(slot_t[:]))
+
+        def round_weight(engine, n, h, t0=0, t1=PACK):
+            src = raw[n, h][:].rearrange("p j (m t) -> p m j t", t=PACK)[:, :, :, t0:t1]
+            dst = w_bf[n][:, t0:t1, h * 64 : (h + 1) * 64, :].rearrange("p t m j -> p m j t")
+            copy_on(engine, dst, src)
+
+        def quantize_weight(n, t0=0, t1=PACK):
+            cols = slice(t0 * P, t1 * P)
+            nc.vector.quantize_mx(
+                out=w_codes[n][:, cols].bitcast(FP8X4),
+                scales=w_scales[n][:, cols],
+                in_=w_bf[n][:, t0:t1, :, :].rearrange("p t m j -> p (t m j)"),
+            )
+
+        def interleave(engine, dst, src):
+            copy_on(
+                engine,
+                dst.rearrange("p (c i) t -> p c t i", i=4),
+                src.rearrange("p t (c i) -> p c t i", i=4),
+            )
+
+        def product(acc, n, t, codes, scales, cols, start):
+            m = slice(t * P, (t + 1) * P)
+            nc.tensor.matmul_mx(
+                out=acc,
+                lhsT=w_codes[n][:, m].bitcast(FP8X4),
+                lhsT_scale=w_scales[n][:, m],
+                rhs=codes[:, cols].bitcast(FP8X4),
+                rhs_scale=scales[:, cols],
+                start=start,
+                stop=not start,
+            )
+
+        gather_mem(0)
+        gather_mem(1)
+        round_weight("scalar", "r2", 0)
+        nc.vector.tensor_copy(x_sc[:], xs_all[:].indirect(offs_t[:]))
+        gather_mem(2)
+        gather_mem(3)
+        interleave("scalar", old_bf[:], old[:])
+        round_weight("vector", "r2", 1)
+        nc.vector.tensor_copy(x_codes[:], xw_all[:].bitcast(U32).indirect(offs_t[:]))
+        quantize_weight("r2")
+        nc.vector.quantize_mx(
+            out=old_codes[:].bitcast(FP8X4), scales=old_scales[:], in_=old_bf[:].rearrange("p s t -> p (s t)")
+        )
+        every = slice(0, S)
+        g_acc = [psum.tile([P, S], F32, name=f"g_acc{t}", tag=f"bank{t}") for t in range(PACK)]
+        for t in range(PACK):
+            product(g_acc[t][:], "r2", t, old_codes, old_scales, every, True)
+        round_weight("scalar", "w2", 0)
+        round_weight("vector", "w2", 1)
+        quantize_weight("w2", 0, 2)
+        quantize_weight("w2", 2, 4)
+        for t in range(PACK):
+            product(g_acc[t][:], "w2", t, x_codes, x_sc, every, False)
+        round_weight("scalar", "w1", 0)
+
+        gg = sb.tile([P, PACK, S], F32, name="gg")
+        diff = sb.tile([P, PACK, S], F32, name="diff")
+        for t in range(PACK):
+            nc.scalar.activation(out=gg[:, t, :], in_=g_acc[t][:], func=TANH, bias=zero[:])
+
+        def make_diff(t):
+            nc.vector.scalar_tensor_tensor(
+                out=diff[:, t, :], in0=old[:, t, :], scalar=unit_t[:, t : t + 1], in1=gg[:, t, :], op0=MULT, op1=SUB
+            )
+
+        round_weight("vector", "w1", 1)
+        make_diff(0)
+        quantize_weight("w1")
+        z_acc = {
+            (h, t): psum.tile([P, S], F32, name=f"z_acc{h}{t}", tag=f"bank{(1 - h) * PACK + t}")
+            for h in range(2)
+            for t in range(PACK)
+        }
+        halves = [slice(h * HALF, (h + 1) * HALF) for h in range(2)]
+        for h in range(2):
+            for t in range(PACK):
+                product(z_acc[h, t][:, 0:HALF], "w1", t, x_codes, x_sc, halves[h], True)
+        round_weight("vector", "r1", 0)
+        round_weight("vector", "r1", 1, 0, 2)
+        round_weight("scalar", "r1", 1, 2, 4)
+        make_diff(1)
+        quantize_weight("r1", 0, 2)
+        quantize_weight("r1", 2, 4)
+        th = sb.tile([P, PACK, S], F32, name="th")
+        for h in range(2):
+            for t in range(PACK):
+                product(z_acc[h, t][:, 0:HALF], "r1", t, old_codes, old_scales, halves[h], False)
+                nc.scalar.activation(
+                    out=th[:, t, halves[h]], in_=z_acc[h, t][:, 0:HALF], func=TANH, bias=zero[:], scale=0.5
+                )
+        make_diff(2)
+        make_diff(3)
+
+        out_rows = out_0.rearrange("(p t) j -> p t j", t=PACK)
+        out_words = out_1[0].rearrange("p c r -> p (c r)").bitcast(I32)
+        y_codes = sb.tile([P, S], I32, name="y_codes", align_bytes=64)
+        y_scales = sb.tile([P, S], U8, name="y_scales", align_bytes=64)
+        chunks = [(0, 256), (256, 384), (384, 512)]
+        e = [sb.tile([P, PACK, b - a], F32, name=f"e{a}") for a, b in chunks]
+        y = [sb.tile([P, PACK, b - a], F32, name=f"y{a}") for a, b in chunks]
+        y_bf = [sb.tile([P, b - a, PACK], BF16, name=f"y_bf{a}", align_bytes=64) for a, b in chunks]
+
+        def gate(c, t0, t1):
+            a, b = chunks[c]
+            nc.vector.scalar_tensor_tensor(
+                out=e[c][:, t0:t1, :], in0=th[:, t0:t1, a:b], scalar=1.0, in1=diff[:, t0:t1, a:b], op0=SUB, op1=MULT
+            )
+
+        def blend(c, t0, t1):
+            a, b = chunks[c]
+            nc.vector.scalar_tensor_tensor(
+                out=y[c][:, t0:t1, :], in0=e[c][:, t0:t1, :], scalar=-0.5, in1=gg[:, t0:t1, a:b], op0=MULT, op1=ADD
+            )
+            nc.sync.dma_start(out_rows[:, t0:t1, a:b], y[c][:, t0:t1, :])
+
+        def quantize_out(c):
+            a, b = chunks[c]
+            nc.vector.quantize_mx(
+                out=y_codes[:, a:b].bitcast(FP8X4),
+                scales=y_scales[:, a:b],
+                in_=y_bf[c][:].rearrange("p s t -> p (s t)"),
+            )
+            nc.sync.dma_start(out_words[:, a:b], y_codes[:, a:b])
+
+        gate(0, 0, 2)
+        gate(0, 2, 4)
+        blend(0, 0, 2)
+        blend(0, 2, 4)
+        interleave("scalar", y_bf[0][:], y[0][:])
+        gate(1, 0, 4)
+        gate(2, 0, 4)
+        blend(1, 0, 4)
+        interleave("scalar", y_bf[1][:], y[1][:])
+        blend(2, 0, 4)
+        quantize_out(0)
+        interleave("vector", y_bf[2][:], y[2][:])
+        quantize_out(1)
+        quantize_out(2)
+        for q in range(4):
+            queue = nc.scalar if q % 2 else nc.sync
+            queue.dma_start(
+                out_2[0, 4 * q : 4 * q + 4, :].bitcast(I32), y_scales[32 * q : 32 * q + 4, :].bitcast(I32)
+            )

@@ -38,21 +38,17 @@ def tile_picked_ytgn_gru_po_kernel(
 
         slot_t = sb.tile([P, S // 16], U16, name="slot_t")
         offs_t = sb.tile([P, S // 16], U16, name="offs_t")
-        nc.sync.dma_start(slot_t[:], slot)
-        nc.sync.dma_start(offs_t[:], offs)
-
         xs_all = sb.tile([P, T], U8, name="xs_all", align_bytes=64)
-        nc.vector.memset(xs_all[:].bitcast(I32), 0)
+        nc.gpsimd.memset(xs_all[:].bitcast(I32), 0)
         for q in range(4):
             nc.scalar.dma_start(
                 xs_all[32 * q : 32 * q + 4, :].bitcast(I32), x_scales[0, 4 * q : 4 * q + 4, :].bitcast(I32)
             )
         unit_t = sb.tile([P, PACK], F32, name="unit_t")
-        nc.scalar.dma_start(unit_t[:], unit.rearrange("(p t) o -> p (t o)", t=PACK))
 
         zero_in = sb.tile([P, 1], F32, name="zero_in")
         zero = sb.tile([P, 1], F32, name="zero")
-        nc.vector.memset(zero_in[:], 0.0)
+        nc.gpsimd.memset(zero_in[:], 0.0)
         nc.scalar.activation(out=zero[:], in_=zero_in[:], func=TANH)
 
         mem_rows = mem.rearrange("(p t) c -> p t c", t=PACK)
@@ -70,13 +66,15 @@ def tile_picked_ytgn_gru_po_kernel(
             rows = weights[n].rearrange("(p j) c -> p j c", j=PACK)
             nc.sync.dma_start(raw[n, h][:], rows[:, :, h * HALF : (h + 1) * HALF])
 
+        nc.sync.dma_start(offs_t[:], offs)
         load_mem(0)
-        load_mem(1)
+        nc.sync.dma_start(slot_t[:], slot)
+        for t in range(1, PACK):
+            load_mem(t)
         load_weight("r2", 0)
-        load_mem(2)
-        load_mem(3)
         load_weight("r2", 1)
         nc.sync.dma_start(xw_all[:], x_words[0].rearrange("p n t -> p (n t)").bitcast(I32))
+        nc.sync.dma_start(unit_t[:], unit.rearrange("(p t) o -> p (t o)", t=PACK))
         for n in ("w2", "w1", "r1"):
             load_weight(n, 0)
             load_weight(n, 1)
@@ -85,9 +83,8 @@ def tile_picked_ytgn_gru_po_kernel(
         old_bf = sb.tile([P, S, PACK], BF16, name="old_bf", align_bytes=64)
         old_codes = sb.tile([P, S], U32, name="old_codes", align_bytes=64)
         old_scales = sb.tile([P, S], U8, name="old_scales", align_bytes=64)
-        x_codes = sb.tile([P, S], U32, name="x_codes", align_bytes=64)
         x_sc = sb.tile([P, S], U8, name="x_sc", align_bytes=64)
-        w_bf = {n: sb.tile([P, PACK, P, PACK], BF16, name=f"bf_{n}", align_bytes=64) for n in weights}
+        w_bf = {n: sb.tile([P, PACK, P, PACK], BF16, name=f"bf_{n}", tag=f"bf_{n}", align_bytes=64) for n in weights}
         w_codes = {n: sb.tile([P, H], U32, name=f"codes_{n}", align_bytes=64) for n in weights}
         w_scales = {n: sb.tile([P, H], U8, name=f"scales_{n}", align_bytes=64) for n in weights}
 
@@ -126,25 +123,24 @@ def tile_picked_ytgn_gru_po_kernel(
                 stop=not start,
             )
 
-        gather_mem(0)
-        gather_mem(1)
-        round_weight("scalar", "r2", 0)
         nc.vector.tensor_copy(x_sc[:], xs_all[:].indirect(offs_t[:]))
-        gather_mem(2)
-        gather_mem(3)
-        interleave("scalar", old_bf[:], old[:])
-        round_weight("vector", "r2", 1)
-        nc.vector.tensor_copy(x_codes[:], xw_all[:].bitcast(U32).indirect(offs_t[:]))
+        for t in range(PACK):
+            gather_mem(t)
+        round_weight("scalar", "r2", 0)
+        round_weight("scalar", "r2", 1)
+        interleave("vector", old_bf[:], old[:])
         quantize_weight("r2")
         nc.vector.quantize_mx(
             out=old_codes[:].bitcast(FP8X4), scales=old_scales[:], in_=old_bf[:].rearrange("p s t -> p (s t)")
         )
+        x_codes = sb.tile([P, S], U32, name="x_codes", tag="bf_r2", align_bytes=64)
+        nc.vector.tensor_copy(x_codes[:], xw_all[:].bitcast(U32).indirect(offs_t[:]))
+        round_weight("scalar", "w2", 0)
         every = slice(0, S)
         g_acc = [psum.tile([P, S], F32, name=f"g_acc{t}", tag=f"bank{t}") for t in range(PACK)]
         for t in range(PACK):
             product(g_acc[t][:], "r2", t, old_codes, old_scales, every, True)
-        round_weight("scalar", "w2", 0)
-        round_weight("vector", "w2", 1)
+        round_weight("scalar", "w2", 1)
         quantize_weight("w2", 0, 2)
         quantize_weight("w2", 2, 4)
         for t in range(PACK):
@@ -152,18 +148,18 @@ def tile_picked_ytgn_gru_po_kernel(
         round_weight("scalar", "w1", 0)
 
         gg = sb.tile([P, PACK, S], F32, name="gg")
-        diff = sb.tile([P, PACK, S], F32, name="diff")
+        diff = [sb.tile([P, 2, S], F32, name="diff_lo")]
         for t in range(PACK):
             nc.scalar.activation(out=gg[:, t, :], in_=g_acc[t][:], func=TANH, bias=zero[:])
 
         def make_diff(t):
             nc.vector.scalar_tensor_tensor(
-                out=diff[:, t, :], in0=old[:, t, :], scalar=unit_t[:, t : t + 1], in1=gg[:, t, :], op0=MULT, op1=SUB
+                out=diff[t // 2][:, t % 2, :], in0=old[:, t, :], scalar=unit_t[:, t : t + 1], in1=gg[:, t, :], op0=MULT, op1=SUB
             )
 
         round_weight("vector", "w1", 1)
-        make_diff(0)
         quantize_weight("w1")
+        make_diff(0)
         z_acc = {
             (h, t): psum.tile([P, S], F32, name=f"z_acc{h}{t}", tag=f"bank{(1 - h) * PACK + t}")
             for h in range(2)
@@ -186,6 +182,7 @@ def tile_picked_ytgn_gru_po_kernel(
                 nc.scalar.activation(
                     out=th[:, t, halves[h]], in_=z_acc[h, t][:, 0:HALF], func=TANH, bias=zero[:], scale=0.5
                 )
+        diff.append(sb.tile([P, 2, S], F32, name="diff_hi", tag="bf_r1", align_bytes=64))
         make_diff(2)
         make_diff(3)
 
@@ -194,20 +191,25 @@ def tile_picked_ytgn_gru_po_kernel(
         y_codes = sb.tile([P, S], I32, name="y_codes", align_bytes=64)
         y_scales = sb.tile([P, S], U8, name="y_scales", align_bytes=64)
         chunks = [(0, 256), (256, 384), (384, 512)]
-        e = [sb.tile([P, PACK, b - a], F32, name=f"e{a}") for a, b in chunks]
+        e = sb.tile([P, PACK, S], F32, name="e")
         y = [sb.tile([P, PACK, b - a], F32, name=f"y{a}") for a, b in chunks]
         y_bf = [sb.tile([P, b - a, PACK], BF16, name=f"y_bf{a}", align_bytes=64) for a, b in chunks]
 
-        def gate(c, t0, t1):
-            a, b = chunks[c]
+        def gate(h, pair):
+            ts = slice(2 * pair, 2 * pair + 2)
             nc.vector.scalar_tensor_tensor(
-                out=e[c][:, t0:t1, :], in0=th[:, t0:t1, a:b], scalar=1.0, in1=diff[:, t0:t1, a:b], op0=SUB, op1=MULT
+                out=e[:, ts, halves[h]],
+                in0=th[:, ts, halves[h]],
+                scalar=1.0,
+                in1=diff[pair][:, :, halves[h]],
+                op0=SUB,
+                op1=MULT,
             )
 
         def blend(c, t0, t1):
             a, b = chunks[c]
             nc.vector.scalar_tensor_tensor(
-                out=y[c][:, t0:t1, :], in0=e[c][:, t0:t1, :], scalar=-0.5, in1=gg[:, t0:t1, a:b], op0=MULT, op1=ADD
+                out=y[c][:, t0:t1, :], in0=e[:, t0:t1, a:b], scalar=-0.5, in1=gg[:, t0:t1, a:b], op0=MULT, op1=ADD
             )
             nc.sync.dma_start(out_rows[:, t0:t1, a:b], y[c][:, t0:t1, :])
 
@@ -220,18 +222,18 @@ def tile_picked_ytgn_gru_po_kernel(
             )
             nc.sync.dma_start(out_words[:, a:b], y_codes[:, a:b])
 
-        gate(0, 0, 2)
-        gate(0, 2, 4)
+        gate(0, 0)
+        gate(0, 1)
         blend(0, 0, 2)
         blend(0, 2, 4)
         interleave("scalar", y_bf[0][:], y[0][:])
-        gate(1, 0, 4)
-        gate(2, 0, 4)
+        gate(1, 0)
+        gate(1, 1)
         blend(1, 0, 4)
         interleave("scalar", y_bf[1][:], y[1][:])
         blend(2, 0, 4)
+        interleave("scalar", y_bf[2][:], y[2][:])
         quantize_out(0)
-        interleave("vector", y_bf[2][:], y[2][:])
         quantize_out(1)
         quantize_out(2)
         for q in range(4):

@@ -1,6 +1,7 @@
 from contextlib import ExitStack
 
 import concourse.mybir as mybir
+from concourse.masks import make_identity
 
 K, T, S, H, U = 512, 1024, 512, 512, 1024
 FLOPS = 4 * 2 * K * H * S
@@ -13,6 +14,7 @@ U16 = mybir.dt.uint16
 U8 = mybir.dt.uint8
 FP8X4 = mybir.dt.float8_e4m3fn_x4
 TANH = mybir.ActivationFunctionType.Tanh
+COPY = mybir.ActivationFunctionType.Copy
 MULT = mybir.AluOpType.mult
 ADD = mybir.AluOpType.add
 SUB = mybir.AluOpType.subtract
@@ -20,6 +22,8 @@ SUB = mybir.AluOpType.subtract
 P = 128
 PACK = 4
 HALF = 256
+CHUNK = 128
+WORDS = HALF // PACK
 
 
 def tile_picked_ytgn_gru_po_kernel(
@@ -39,25 +43,53 @@ def tile_picked_ytgn_gru_po_kernel(
         slot_t = sb.tile([P, S // 16], U16, name="slot_t")
         offs_t = sb.tile([P, S // 16], U16, name="offs_t")
         xs_all = sb.tile([P, T], U8, name="xs_all", align_bytes=64)
-        nc.gpsimd.memset(xs_all[:].bitcast(I32), 0)
-        for q in range(4):
-            nc.scalar.dma_start(
-                xs_all[32 * q : 32 * q + 4, :].bitcast(I32), x_scales[0, 4 * q : 4 * q + 4, :].bitcast(I32)
-            )
+        xw_all = sb.tile([P, T], I32, name="xw_all", align_bytes=64)
         unit_t = sb.tile([P, PACK], F32, name="unit_t")
-
         zero_in = sb.tile([P, 1], F32, name="zero_in")
         zero = sb.tile([P, 1], F32, name="zero")
-        nc.gpsimd.memset(zero_in[:], 0.0)
-        nc.scalar.activation(out=zero[:], in_=zero_in[:], func=TANH)
-
+        ident = sb.tile([P, P], F32, name="ident")
         mem_rows = mem.rearrange("(p t) c -> p t c", t=PACK)
-        mem_t = [sb.tile([P, U], F32, name=f"mem{t}") for t in range(PACK)]
+        mem_t = [sb.tile([P, U], F32, name=f"mem{t}", tag=f"mem{t}") for t in range(PACK)]
         weights = {"w1": w1, "w2": w2, "r1": r1, "r2": r2}
-        raw = {
-            (n, h): sb.tile([P, PACK, HALF], F32, name=f"raw_{n}_{h}") for n in weights for h in range(2)
+        pieces = [(n, h) for n in weights for h in range(2)]
+        raw = {k: sb.tile([P, PACK, HALF], F32, name=f"raw_{k[0]}_{k[1]}", tag=f"raw_{k[0]}_{k[1]}") for k in pieces}
+        w_bf = {
+            k: sb.tile([P, PACK, WORDS, PACK], BF16, name=f"bf_{k[0]}_{k[1]}", tag=f"bf_{k[0]}_{k[1]}", align_bytes=64)
+            for k in pieces
         }
-        xw_all = sb.tile([P, T], I32, name="xw_all", align_bytes=64)
+        w_codes = {k: sb.tile([P, HALF], U32, name=f"codes_{k[0]}_{k[1]}", align_bytes=64) for k in pieces}
+        w_scales = {k: sb.tile([P, HALF], U8, name=f"scales_{k[0]}_{k[1]}", align_bytes=64) for k in pieces}
+        old = sb.tile([P, PACK, S], F32, name="old")
+        ov = sb.tile([P, PACK, S], F32, name="ov")
+        unit_half = sb.tile([P, PACK], F32, name="unit_half")
+        old_bf = [sb.tile([P, 2, CHUNK, PACK], BF16, name=f"old_bf{c}", align_bytes=64) for c in range(2)]
+        old_codes = [sb.tile([P, 2, CHUNK], U32, name=f"old_codes{c}", align_bytes=64) for c in range(2)]
+        old_scales = [sb.tile([P, 2, CHUNK], U8, name=f"old_scales{c}", align_bytes=64) for c in range(2)]
+        x_sc = sb.tile([P, S], U8, name="x_sc", align_bytes=64)
+        blocks = [(h, c) for h in range(2) for c in range(2)]
+        gg = {}
+        th = {b: sb.tile([P, PACK, 2, WORDS], F32, name=f"th{b[0]}{b[1]}") for b in blocks}
+        diff = {}
+        gated = {}
+        y = {}
+        y_bf = {b: sb.tile([P, CHUNK, PACK], BF16, name=f"y_bf{b[0]}{b[1]}", align_bytes=64) for b in blocks}
+        y_codes = sb.tile([P, 2, HALF], I32, name="y_codes", align_bytes=64)
+        y_scales = sb.tile([P, HALF], U8, name="y_scales", align_bytes=64)
+        out_rows = out_0.rearrange("(h m t) (g j) -> h g m t j", h=2, t=PACK, g=2)
+        out_words = out_1[0].rearrange("p c r -> p (c r)").bitcast(I32).rearrange("(h m) (g j) -> g m h j", h=2, g=2)
+        out_scales = out_2[0].bitcast(I32).rearrange("(h a r) (g c) -> a g h r c", h=2, a=2, g=2)
+        ov_turned = {}
+        g_acc = {}
+        z_acc = {}
+        y_acc = {}
+
+        def cols_of(g, c):
+            return slice(g * HALF + c * CHUNK, g * HALF + (c + 1) * CHUNK)
+
+        def load_scales(queue, q):
+            queue.dma_start(
+                xs_all[32 * q : 32 * q + 4, :].bitcast(I32), x_scales[0, 4 * q : 4 * q + 4, :].bitcast(I32)
+            )
 
         def load_mem(t):
             nc.sync.dma_start(mem_t[t][:], mem_rows[:, t, :])
@@ -66,42 +98,50 @@ def tile_picked_ytgn_gru_po_kernel(
             rows = weights[n].rearrange("(p j) c -> p j c", j=PACK)
             nc.sync.dma_start(raw[n, h][:], rows[:, :, h * HALF : (h + 1) * HALF])
 
-        nc.sync.dma_start(offs_t[:], offs)
-        load_mem(0)
-        nc.sync.dma_start(slot_t[:], slot)
-        for t in range(1, PACK):
-            load_mem(t)
-        load_weight("r2", 0)
-        load_weight("r2", 1)
-        nc.sync.dma_start(xw_all[:], x_words[0].rearrange("p n t -> p (n t)").bitcast(I32))
-        nc.sync.dma_start(unit_t[:], unit.rearrange("(p t) o -> p (t o)", t=PACK))
-        for n in ("w2", "w1", "r1"):
-            load_weight(n, 0)
-            load_weight(n, 1)
+        def load_x():
+            nc.sync.dma_start(xw_all[:], x_words[0].rearrange("p n t -> p (n t)").bitcast(I32))
 
-        old = sb.tile([P, PACK, S], F32, name="old")
-        old_bf = sb.tile([P, S, PACK], BF16, name="old_bf", align_bytes=64)
-        old_codes = sb.tile([P, S], U32, name="old_codes", align_bytes=64)
-        old_scales = sb.tile([P, S], U8, name="old_scales", align_bytes=64)
-        x_sc = sb.tile([P, S], U8, name="x_sc", align_bytes=64)
-        w_bf = {n: sb.tile([P, PACK, P, PACK], BF16, name=f"bf_{n}", tag=f"bf_{n}", align_bytes=64) for n in weights}
-        w_codes = {n: sb.tile([P, H], U32, name=f"codes_{n}", align_bytes=64) for n in weights}
-        w_scales = {n: sb.tile([P, H], U8, name=f"scales_{n}", align_bytes=64) for n in weights}
+        def load_unit():
+            nc.sync.dma_start(unit_t[:], unit.rearrange("(p t) o -> p (t o)", t=PACK))
 
-        def gather_mem(t):
-            nc.vector.tensor_copy(old[:, t, :], mem_t[t][:].indirect(slot_t[:]))
+        def gather_mem(engine, t, a=0, b=S):
+            window = mem_t[t][:].indirect(slot_t[:, a // 16 : b // 16])
+            if engine == "scalar":
+                nc.scalar.activation(out=old[:, t, a:b], in_=window, func=COPY)
+            else:
+                nc.vector.tensor_copy(old[:, t, a:b], window)
 
-        def round_weight(engine, n, h, t0=0, t1=PACK):
-            src = raw[n, h][:].rearrange("p j (m t) -> p m j t", t=PACK)[:, :, :, t0:t1]
-            dst = w_bf[n][:, t0:t1, h * 64 : (h + 1) * 64, :].rearrange("p t m j -> p m j t")
+        def gather_x_words():
+            nc.vector.tensor_copy(x_codes[:], xw_all[:].bitcast(U32).indirect(offs_t[:]))
+
+        def gather_x_scales():
+            nc.vector.tensor_copy(x_sc[:], xs_all[:].indirect(offs_t[:]))
+
+        def scale_old(t):
+            nc.gpsimd.tensor_scalar(
+                out=ov[:, t, :], in0=old[:, t, :], scalar1=unit_half[:, t : t + 1], scalar2=0.0, op0=MULT, op1=ADD
+            )
+
+        def turn_ov(g, c):
+            bank = psum.tile([P, PACK, P], F32, name=f"ov_turned{g}{c}", tag=f"bank{2 * c + g}")
+            ov_turned[g, c] = bank
+            for t in range(PACK):
+                nc.tensor.transpose(bank[:, t, :], ov[:, t, cols_of(g, c)], ident[:])
+
+        def round_weight(engine, n, h, m0=0, m1=WORDS):
+            src = raw[n, h][:, :, PACK * m0 : PACK * m1].rearrange("p j (m t) -> p m j t", t=PACK)
+            dst = w_bf[n, h][:, :, m0:m1, :].rearrange("p t m j -> p m j t")
             copy_on(engine, dst, src)
 
-        def quantize_weight(n, t0=0, t1=PACK):
-            cols = slice(t0 * P, t1 * P)
+        def prepare(engine, n, h):
+            round_weight(engine, n, h)
+            quantize_weight(n, h)
+
+        def quantize_weight(n, h):
             nc.vector.quantize_mx(
-                out=w_codes[n][:, cols].bitcast(FP8X4),
-                scales=w_scales[n][:, cols],
-                in_=w_bf[n][:, t0:t1, :, :].rearrange("p t m j -> p (t m j)"),
+                out=w_codes[n, h][:].bitcast(FP8X4),
+                scales=w_scales[n, h][:],
+                in_=w_bf[n, h][:].rearrange("p t m j -> p (t m j)"),
             )
 
         def interleave(engine, dst, src):
@@ -111,133 +151,201 @@ def tile_picked_ytgn_gru_po_kernel(
                 src.rearrange("p t (c i) -> p c t i", i=4),
             )
 
-        def product(acc, n, t, codes, scales, cols, start):
-            m = slice(t * P, (t + 1) * P)
-            nc.tensor.matmul_mx(
-                out=acc,
-                lhsT=w_codes[n][:, m].bitcast(FP8X4),
-                lhsT_scale=w_scales[n][:, m],
-                rhs=codes[:, cols].bitcast(FP8X4),
-                rhs_scale=scales[:, cols],
-                start=start,
-                stop=not start,
+        def round_old(engine, c):
+            src = old[:].rearrange("p t (g c a i) -> p c g a t i", g=2, c=2, i=4)[:, c]
+            copy_on(engine, old_bf[c][:].rearrange("p g (a i) t -> p g a t i", i=4), src)
+
+        def quantize_old(c):
+            nc.vector.quantize_mx(
+                out=old_codes[c][:].rearrange("p g j -> p (g j)").bitcast(FP8X4),
+                scales=old_scales[c][:].rearrange("p g j -> p (g j)"),
+                in_=old_bf[c][:].rearrange("p g j t -> p (g j t)"),
             )
 
-        nc.vector.tensor_copy(x_sc[:], xs_all[:].indirect(offs_t[:]))
-        for t in range(PACK):
-            gather_mem(t)
-        round_weight("scalar", "r2", 0)
-        round_weight("scalar", "r2", 1)
-        interleave("vector", old_bf[:], old[:])
-        quantize_weight("r2")
-        nc.vector.quantize_mx(
-            out=old_codes[:].bitcast(FP8X4), scales=old_scales[:], in_=old_bf[:].rearrange("p s t -> p (s t)")
-        )
-        x_codes = sb.tile([P, S], U32, name="x_codes", tag="bf_r2", align_bytes=64)
-        nc.vector.tensor_copy(x_codes[:], xw_all[:].bitcast(U32).indirect(offs_t[:]))
-        round_weight("scalar", "w2", 0)
-        every = slice(0, S)
-        g_acc = [psum.tile([P, S], F32, name=f"g_acc{t}", tag=f"bank{t}") for t in range(PACK)]
-        for t in range(PACK):
-            product(g_acc[t][:], "r2", t, old_codes, old_scales, every, True)
-        round_weight("scalar", "w2", 1)
-        quantize_weight("w2", 0, 2)
-        quantize_weight("w2", 2, 4)
-        for t in range(PACK):
-            product(g_acc[t][:], "w2", t, x_codes, x_sc, every, False)
-        round_weight("scalar", "w1", 0)
-
-        gg = sb.tile([P, PACK, S], F32, name="gg")
-        diff = [sb.tile([P, 2, S], F32, name="diff_lo")]
-        for t in range(PACK):
-            nc.scalar.activation(out=gg[:, t, :], in_=g_acc[t][:], func=TANH, bias=zero[:])
-
-        def make_diff(t):
-            nc.vector.scalar_tensor_tensor(
-                out=diff[t // 2][:, t % 2, :], in0=old[:, t, :], scalar=unit_t[:, t : t + 1], in1=gg[:, t, :], op0=MULT, op1=SUB
-            )
-
-        round_weight("vector", "w1", 1)
-        quantize_weight("w1")
-        make_diff(0)
-        z_acc = {
-            (h, t): psum.tile([P, S], F32, name=f"z_acc{h}{t}", tag=f"bank{(1 - h) * PACK + t}")
-            for h in range(2)
-            for t in range(PACK)
-        }
-        halves = [slice(h * HALF, (h + 1) * HALF) for h in range(2)]
-        for h in range(2):
-            for t in range(PACK):
-                product(z_acc[h, t][:, 0:HALF], "w1", t, x_codes, x_sc, halves[h], True)
-        round_weight("vector", "r1", 0)
-        round_weight("vector", "r1", 1, 0, 2)
-        round_weight("scalar", "r1", 1, 2, 4)
-        make_diff(1)
-        quantize_weight("r1", 0, 2)
-        quantize_weight("r1", 2, 4)
-        th = sb.tile([P, PACK, S], F32, name="th")
-        for h in range(2):
-            for t in range(PACK):
-                product(z_acc[h, t][:, 0:HALF], "r1", t, old_codes, old_scales, halves[h], False)
-                nc.scalar.activation(
-                    out=th[:, t, halves[h]], in_=z_acc[h, t][:, 0:HALF], func=TANH, bias=zero[:], scale=0.5
+        def products(acc, n, h, c, first):
+            for g in range(2):
+                if n in ("w1", "w2"):
+                    codes, scales = x_codes[:, cols_of(g, c)], x_sc[:, cols_of(g, c)]
+                else:
+                    codes, scales = old_codes[c][:, g, :], old_scales[c][:, g, :]
+                nc.tensor.matmul_mx(
+                    out=acc[h, c][:, g, :],
+                    lhsT=codes.bitcast(FP8X4),
+                    lhsT_scale=scales,
+                    rhs=w_codes[n, h][:].bitcast(FP8X4),
+                    rhs_scale=w_scales[n, h][:],
+                    start=first and g == 0,
+                    stop=not first and g == 1,
                 )
-        diff.append(sb.tile([P, 2, S], F32, name="diff_hi", tag="bf_r1", align_bytes=64))
-        make_diff(2)
-        make_diff(3)
 
-        out_rows = out_0.rearrange("(p t) j -> p t j", t=PACK)
-        out_words = out_1[0].rearrange("p c r -> p (c r)").bitcast(I32)
-        y_codes = sb.tile([P, S], I32, name="y_codes", align_bytes=64)
-        y_scales = sb.tile([P, S], U8, name="y_scales", align_bytes=64)
-        chunks = [(0, 256), (256, 384), (384, 512)]
-        e = sb.tile([P, PACK, S], F32, name="e")
-        y = [sb.tile([P, PACK, b - a], F32, name=f"y{a}") for a, b in chunks]
-        y_bf = [sb.tile([P, b - a, PACK], BF16, name=f"y_bf{a}", align_bytes=64) for a, b in chunks]
+        def open_sum(acc, name, n, h, c, bank):
+            acc[h, c] = psum.tile([P, 2, HALF], F32, name=f"{name}{h}{c}", tag=f"bank{bank}")
+            products(acc, n, h, c, True)
 
-        def gate(h, pair):
-            ts = slice(2 * pair, 2 * pair + 2)
+        def tanh_of(dst, acc, scale):
+            nc.scalar.activation(
+                out=dst[:],
+                in_=acc[:].rearrange("p g (t m) -> p t g m", t=PACK),
+                func=TANH,
+                bias=zero[:],
+                scale=scale,
+            )
+
+        def turn_add(h, c, src, first):
+            for t in range(PACK):
+                nc.tensor.matmul(
+                    y_acc[h, c][:, t, :],
+                    src[:, t].rearrange("p g m -> p (g m)"),
+                    ident[:],
+                    start=first and t == 0,
+                    stop=not first and t == PACK - 1,
+                    is_transpose=True,
+                )
+
+        def candidate(h, tag):
+            pair = sb.tile([P, 2, PACK, 2, WORDS], F32, name=f"gg{h}", tag=tag)
+            for c in range(2):
+                gg[h, c] = pair[:, c]
+                tanh_of(gg[h, c], g_acc[h, c], 1.0)
+
+        def open_result(h, c, bank):
+            y_acc[h, c] = psum.tile([P, PACK, CHUNK], F32, name=f"y_acc{h}{c}", tag=f"bank{bank}")
+            turn_add(h, c, gg[h, c], True)
+
+        def make_diff(h, c, tag):
+            diff[h, c] = sb.tile([P, PACK, 2, WORDS], F32, name=f"diff{h}{c}", tag=tag, align_bytes=64)
+            for g in range(2):
+                nc.vector.scalar_tensor_tensor(
+                    out=diff[h, c][:, :, g, :],
+                    in0=gg[h, c][:, :, g, :],
+                    scalar=0.5,
+                    in1=ov_turned[g, c][:, :, h * WORDS : (h + 1) * WORDS],
+                    op0=MULT,
+                    op1=ADD,
+                )
+
+        def gate_tanh(h, c):
+            products(z_acc, "r1", h, c, False)
+            tanh_of(th[h, c], z_acc[h, c], 0.5)
+
+        def gate(h, c, tag):
+            gated[h, c] = sb.tile([P, PACK, 2, WORDS], F32, name=f"gated{h}{c}", tag=tag, align_bytes=64)
             nc.vector.scalar_tensor_tensor(
-                out=e[:, ts, halves[h]],
-                in0=th[:, ts, halves[h]],
+                out=gated[h, c][:].rearrange("p t g m -> p (t g m)"),
+                in0=th[h, c][:].rearrange("p t g m -> p (t g m)"),
                 scalar=1.0,
-                in1=diff[pair][:, :, halves[h]],
+                in1=diff[h, c][:].rearrange("p t g m -> p (t g m)"),
                 op0=SUB,
                 op1=MULT,
             )
+            turn_add(h, c, gated[h, c], False)
 
-        def blend(c, t0, t1):
-            a, b = chunks[c]
-            nc.vector.scalar_tensor_tensor(
-                out=y[c][:, t0:t1, :], in0=e[:, t0:t1, a:b], scalar=-0.5, in1=gg[:, t0:t1, a:b], op0=MULT, op1=ADD
-            )
-            nc.sync.dma_start(out_rows[:, t0:t1, a:b], y[c][:, t0:t1, :])
+        def take_out(engine, h, c, tag):
+            y[h, c] = sb.tile([P, PACK, CHUNK], F32, name=f"y{h}{c}", tag=tag, align_bytes=64)
+            copy_on(engine, y[h, c][:], y_acc[h, c][:])
+            for g in range(2):
+                nc.sync.dma_start(
+                    out_rows[h, g][:, :, c * CHUNK : (c + 1) * CHUNK], y[h, c][g * WORDS : (g + 1) * WORDS]
+                )
 
-        def quantize_out(c):
-            a, b = chunks[c]
+        def round_out(engine, h, c):
+            interleave(engine, y_bf[h, c][:], y[h, c][:])
+
+        def quantize_out(h, c):
+            cols = slice(c * CHUNK, (c + 1) * CHUNK)
             nc.vector.quantize_mx(
-                out=y_codes[:, a:b].bitcast(FP8X4),
-                scales=y_scales[:, a:b],
-                in_=y_bf[c][:].rearrange("p s t -> p (s t)"),
+                out=y_codes[:, h, cols].bitcast(FP8X4),
+                scales=y_scales[4 * h :, cols],
+                in_=y_bf[h, c][:].rearrange("p s t -> p (s t)"),
             )
-            nc.sync.dma_start(out_words[:, a:b], y_codes[:, a:b])
 
-        gate(0, 0)
-        gate(0, 1)
-        blend(0, 0, 2)
-        blend(0, 2, 4)
-        interleave("scalar", y_bf[0][:], y[0][:])
-        gate(1, 0)
-        gate(1, 1)
-        blend(1, 0, 4)
-        interleave("scalar", y_bf[1][:], y[1][:])
-        blend(2, 0, 4)
-        interleave("scalar", y_bf[2][:], y[2][:])
-        quantize_out(0)
-        quantize_out(1)
-        quantize_out(2)
+        def store_words():
+            for g, queue in enumerate((nc.sync, nc.scalar)):
+                queue.dma_start(out_words[g], y_codes[g * WORDS : (g + 1) * WORDS])
+
+        def store_scales():
+            for q in range(4):
+                queue = nc.sync if q % 2 else nc.scalar
+                queue.dma_start(out_scales[q % 2, q // 2], y_scales[32 * q : 32 * q + 8, :].bitcast(I32))
+
+        nc.vector.memset(xs_all[:].bitcast(I32), 0)
+        nc.vector.memset(zero_in[:], 0.0)
+        nc.scalar.activation(out=zero[:], in_=zero_in[:], func=TANH)
+        make_identity(nc, ident[:])
+        nc.sync.dma_start(slot_t[:], slot)
+        nc.sync.dma_start(offs_t[:], offs)
+        load_mem(0)
         for q in range(4):
-            queue = nc.scalar if q % 2 else nc.sync
-            queue.dma_start(
-                out_2[0, 4 * q : 4 * q + 4, :].bitcast(I32), y_scales[32 * q : 32 * q + 4, :].bitcast(I32)
-            )
+            load_scales(nc.sync, q)
+        load_mem(1)
+        load_unit()
+        load_mem(2)
+        load_mem(3)
+        load_weight("r2", 0)
+        load_x()
+        for n, h in (("w2", 0), ("w1", 0), ("r1", 0), ("r2", 1), ("w2", 1), ("w1", 1), ("r1", 1)):
+            load_weight(n, h)
+
+        both = range(2)
+        gather_mem("scalar", 0)
+        gather_x_scales()
+        gather_mem("vector", 1)
+        gather_mem("scalar", 2)
+        gather_mem("vector", 3, 0, HALF)
+        gather_mem("scalar", 3, HALF, S)
+        nc.gpsimd.tensor_scalar(out=unit_half[:], in0=unit_t[:], scalar1=-0.5, scalar2=0.0, op0=MULT, op1=ADD)
+        for t in range(PACK):
+            scale_old(t)
+        for c in both:
+            round_old("vector", c)
+        for c in both:
+            quantize_old(c)
+        prepare("scalar", "r2", 0)
+        for c in both:
+            open_sum(g_acc, "g_acc", "r2", 0, c, 4 + c)
+        x_codes = sb.tile([P, S], U32, name="x_codes", tag="bf_r2_0", align_bytes=64)
+        gather_x_words()
+        prepare("scalar", "w2", 0)
+        for c in both:
+            products(g_acc, "w2", 0, c, False)
+        candidate(0, "gg0")
+        prepare("scalar", "w1", 0)
+        prepare("vector", "r1", 0)
+        for c in both:
+            open_sum(z_acc, "z_acc", "w1", 0, c, 6 + c)
+        prepare("scalar", "r2", 1)
+        prepare("vector", "w2", 1)
+        for c in both:
+            gate_tanh(0, c)
+        for c in both:
+            open_sum(g_acc, "g_acc", "r2", 1, c, 6 + c)
+            products(g_acc, "w2", 1, c, False)
+        candidate(1, "gg1")
+        prepare("scalar", "w1", 1)
+        prepare("vector", "r1", 1)
+        for c in both:
+            open_sum(z_acc, "z_acc", "w1", 1, c, 6 + c)
+            gate_tanh(1, c)
+        for c in both:
+            for g in both:
+                turn_ov(g, c)
+        for c in both:
+            make_diff(0, c, f"diff0{c}")
+            open_result(0, c, 4 + c)
+        for c in both:
+            make_diff(1, c, f"diff1{c}")
+            open_result(1, c, 2 * c)
+        gate(0, 0, "gated00")
+        gate(0, 1, "gated01")
+        gate(1, 0, "gated10")
+        gate(1, 1, "gated11")
+        take_out("scalar", 0, 0, "y00")
+        take_out("scalar", 0, 1, "y01")
+        for c in both:
+            take_out("scalar", 1, c, f"y1{c}")
+        for h in both:
+            for c in both:
+                round_out("vector", h, c)
+                quantize_out(h, c)
+        store_words()
+        store_scales()

@@ -54,13 +54,13 @@ def tile_picked_ytgn_gru_po_kernel(
         pieces = [(n, h) for n in weights for h in range(2)]
         raw = {k: sb.tile([P, PACK, HALF], F32, name=f"raw_{k[0]}_{k[1]}", tag=f"raw_{k[0]}_{k[1]}") for k in pieces}
         w_bf = {
-            k: sb.tile([P, PACK, WORDS, PACK], BF16, name=f"bf_{k[0]}_{k[1]}", tag=f"bf_{k[0]}_{k[1]}", align_bytes=64)
+            k: sb.tile([P, HALF, PACK], BF16, name=f"bf_{k[0]}_{k[1]}", tag=f"bf_{k[0]}_{k[1]}", align_bytes=64)
             for k in pieces
         }
         w_codes = {k: sb.tile([P, HALF], U32, name=f"codes_{k[0]}_{k[1]}", align_bytes=64) for k in pieces}
         w_scales = {k: sb.tile([P, HALF], U8, name=f"scales_{k[0]}_{k[1]}", align_bytes=64) for k in pieces}
         old = sb.tile([P, PACK, S], F32, name="old")
-        ov = sb.tile([P, PACK, S], F32, name="ov")
+        ov = {}
         unit_half = sb.tile([P, PACK], F32, name="unit_half")
         old_bf = [sb.tile([P, 2, CHUNK, PACK], BF16, name=f"old_bf{c}", align_bytes=64) for c in range(2)]
         old_codes = [sb.tile([P, 2, CHUNK], U32, name=f"old_codes{c}", align_bytes=64) for c in range(2)]
@@ -71,7 +71,7 @@ def tile_picked_ytgn_gru_po_kernel(
         th = {b: sb.tile([P, PACK, 2, WORDS], F32, name=f"th{b[0]}{b[1]}") for b in blocks}
         diff = {}
         gated = {}
-        y = {}
+        y = [sb.tile([P, PACK, 2, CHUNK], F32, name=f"y{h}") for h in range(2)]
         y_bf = {b: sb.tile([P, CHUNK, PACK], BF16, name=f"y_bf{b[0]}{b[1]}", align_bytes=64) for b in blocks}
         y_codes = sb.tile([P, 2, HALF], I32, name="y_codes", align_bytes=64)
         y_scales = sb.tile([P, HALF], U8, name="y_scales", align_bytes=64)
@@ -117,21 +117,24 @@ def tile_picked_ytgn_gru_po_kernel(
         def gather_x_scales():
             nc.vector.tensor_copy(x_sc[:], xs_all[:].indirect(offs_t[:]))
 
-        def scale_old(t):
-            nc.gpsimd.tensor_scalar(
-                out=ov[:, t, :], in0=old[:, t, :], scalar1=unit_half[:, t : t + 1], scalar2=0.0, op0=MULT, op1=ADD
-            )
+        def scale_old(engine, t, tag):
+            ov[t] = sb.tile([P, S], F32, name=f"ov{t}", tag=tag)
+            dst = ov[t][:]
+            if engine == "scalar":
+                nc.scalar.activation(out=dst, in_=old[:, t, :], func=COPY, scale=unit_half[:, t : t + 1])
+            else:
+                nc.vector.tensor_scalar(
+                    out=dst, in0=old[:, t, :], scalar1=unit_half[:, t : t + 1], scalar2=None, op0=MULT
+                )
 
         def turn_ov(g, c):
             bank = psum.tile([P, PACK, P], F32, name=f"ov_turned{g}{c}", tag=f"bank{2 * c + g}")
             ov_turned[g, c] = bank
             for t in range(PACK):
-                nc.tensor.transpose(bank[:, t, :], ov[:, t, cols_of(g, c)], ident[:])
+                nc.tensor.transpose(bank[:, t, :], ov[t][:, cols_of(g, c)], ident[:])
 
-        def round_weight(engine, n, h, m0=0, m1=WORDS):
-            src = raw[n, h][:, :, PACK * m0 : PACK * m1].rearrange("p j (m t) -> p m j t", t=PACK)
-            dst = w_bf[n, h][:, :, m0:m1, :].rearrange("p t m j -> p m j t")
-            copy_on(engine, dst, src)
+        def round_weight(engine, n, h):
+            interleave(engine, w_bf[n, h][:], raw[n, h][:])
 
         def prepare(engine, n, h):
             round_weight(engine, n, h)
@@ -141,7 +144,7 @@ def tile_picked_ytgn_gru_po_kernel(
             nc.vector.quantize_mx(
                 out=w_codes[n, h][:].bitcast(FP8X4),
                 scales=w_scales[n, h][:],
-                in_=w_bf[n, h][:].rearrange("p t m j -> p (t m j)"),
+                in_=w_bf[n, h][:].rearrange("p c j -> p (c j)"),
             )
 
         def interleave(engine, dst, src):
@@ -184,8 +187,8 @@ def tile_picked_ytgn_gru_po_kernel(
 
         def tanh_of(dst, acc, scale):
             nc.scalar.activation(
-                out=dst[:],
-                in_=acc[:].rearrange("p g (t m) -> p t g m", t=PACK),
+                out=dst.rearrange("p t g m -> p t (g m)"),
+                in_=acc[:].rearrange("p g (m t) -> p t (g m)", t=PACK),
                 func=TANH,
                 bias=zero[:],
                 scale=scale,
@@ -226,7 +229,7 @@ def tile_picked_ytgn_gru_po_kernel(
 
         def gate_tanh(h, c):
             products(z_acc, "r1", h, c, False)
-            tanh_of(th[h, c], z_acc[h, c], 0.5)
+            tanh_of(th[h, c][:], z_acc[h, c], 0.5)
 
         def gate(h, c, tag):
             gated[h, c] = sb.tile([P, PACK, 2, WORDS], F32, name=f"gated{h}{c}", tag=tag, align_bytes=64)
@@ -240,16 +243,15 @@ def tile_picked_ytgn_gru_po_kernel(
             )
             turn_add(h, c, gated[h, c], False)
 
-        def take_out(engine, h, c, tag):
-            y[h, c] = sb.tile([P, PACK, CHUNK], F32, name=f"y{h}{c}", tag=tag, align_bytes=64)
-            copy_on(engine, y[h, c][:], y_acc[h, c][:])
-            for g in range(2):
-                nc.sync.dma_start(
-                    out_rows[h, g][:, :, c * CHUNK : (c + 1) * CHUNK], y[h, c][g * WORDS : (g + 1) * WORDS]
-                )
+        def take_out(engine, h, c):
+            copy_on(engine, y[h][:, :, c, :], y_acc[h, c][:])
+
+        def store_rows(h):
+            for g, queue in enumerate((nc.sync, nc.scalar)):
+                queue.dma_start(out_rows[h, g], y[h][g * WORDS : (g + 1) * WORDS].rearrange("p t c j -> p t (c j)"))
 
         def round_out(engine, h, c):
-            interleave(engine, y_bf[h, c][:], y[h, c][:])
+            interleave(engine, y_bf[h, c][:], y[h][:, :, c, :])
 
         def quantize_out(h, c):
             cols = slice(c * CHUNK, (c + 1) * CHUNK)
@@ -259,9 +261,9 @@ def tile_picked_ytgn_gru_po_kernel(
                 in_=y_bf[h, c][:].rearrange("p s t -> p (s t)"),
             )
 
-        def store_words():
-            for g, queue in enumerate((nc.sync, nc.scalar)):
-                queue.dma_start(out_words[g], y_codes[g * WORDS : (g + 1) * WORDS])
+        def store_words(h, queues):
+            for g, queue in enumerate(queues):
+                queue.dma_start(out_words[g][:, h, :], y_codes[g * WORDS : (g + 1) * WORDS, h, :])
 
         def store_scales():
             for q in range(4):
@@ -294,8 +296,8 @@ def tile_picked_ytgn_gru_po_kernel(
         gather_mem("vector", 3, 0, HALF)
         gather_mem("scalar", 3, HALF, S)
         nc.gpsimd.tensor_scalar(out=unit_half[:], in0=unit_t[:], scalar1=-0.5, scalar2=0.0, op0=MULT, op1=ADD)
-        for t in range(PACK):
-            scale_old(t)
+        scale_old("scalar", 0, "ov0")
+        scale_old("vector", 1, "ov1")
         for c in both:
             round_old("vector", c)
         for c in both:
@@ -305,6 +307,8 @@ def tile_picked_ytgn_gru_po_kernel(
             open_sum(g_acc, "g_acc", "r2", 0, c, 4 + c)
         x_codes = sb.tile([P, S], U32, name="x_codes", tag="bf_r2_0", align_bytes=64)
         gather_x_words()
+        scale_old("scalar", 2, "mem3")
+        scale_old("vector", 3, "ov3")
         prepare("scalar", "w2", 0)
         for c in both:
             products(g_acc, "w2", 0, c, False)
@@ -339,13 +343,13 @@ def tile_picked_ytgn_gru_po_kernel(
         gate(0, 1, "gated01")
         gate(1, 0, "gated10")
         gate(1, 1, "gated11")
-        take_out("scalar", 0, 0, "y00")
-        take_out("scalar", 0, 1, "y01")
-        for c in both:
-            take_out("scalar", 1, c, f"y1{c}")
+        for h in both:
+            for c in both:
+                take_out("scalar", h, c)
+            store_rows(h)
         for h in both:
             for c in both:
                 round_out("vector", h, c)
                 quantize_out(h, c)
-        store_words()
+            store_words(h, (nc.sync, nc.scalar if h else nc.sync))
         store_scales()

@@ -68,11 +68,13 @@ def tile_picked_ytgn_gru_po_kernel(
         x_sc = sb.tile([P, S], U8, name="x_sc", align_bytes=64)
         blocks = [(h, c) for h in range(2) for c in range(2)]
         gg = {}
-        th = {b: sb.tile([P, PACK, 2, WORDS], F32, name=f"th{b[0]}{b[1]}") for b in blocks}
+        th = {
+            b: sb.tile([P, PACK, 2, WORDS], F32, name=f"th{b[0]}{b[1]}", tag=f"th{b[0]}{b[1]}", align_bytes=64)
+            for b in blocks
+        }
         diff = {}
-        gated = {}
+        gated = {b: sb.tile([P, PACK, 2, WORDS], F32, name=f"gated{b[0]}{b[1]}") for b in blocks}
         y = [sb.tile([P, PACK, 2, CHUNK], F32, name=f"y{h}") for h in range(2)]
-        y_bf = {b: sb.tile([P, CHUNK, PACK], BF16, name=f"y_bf{b[0]}{b[1]}", align_bytes=64) for b in blocks}
         y_codes = sb.tile([P, 2, HALF], I32, name="y_codes", align_bytes=64)
         y_scales = sb.tile([P, HALF], U8, name="y_scales", align_bytes=64)
         out_rows = out_0.rearrange("(h m t) (g j) -> h g m t j", h=2, t=PACK, g=2)
@@ -185,23 +187,23 @@ def tile_picked_ytgn_gru_po_kernel(
             acc[h, c] = psum.tile([P, 2, HALF], F32, name=f"{name}{h}{c}", tag=f"bank{bank}")
             products(acc, n, h, c, True)
 
-        def tanh_of(dst, acc, scale):
+        def tanh_of(dst, acc, scale, t0=0, t1=PACK):
             nc.scalar.activation(
-                out=dst.rearrange("p t g m -> p t (g m)"),
-                in_=acc[:].rearrange("p g (m t) -> p t (g m)", t=PACK),
+                out=dst[:, t0:t1].rearrange("p t g m -> p t (g m)"),
+                in_=acc[:].rearrange("p g (m t) -> p t (g m)", t=PACK)[:, t0:t1],
                 func=TANH,
                 bias=zero[:],
                 scale=scale,
             )
 
-        def turn_add(h, c, src, first):
-            for t in range(PACK):
+        def turn_add(h, c, src, first, t0, t1):
+            for t in range(t0, t1):
                 nc.tensor.matmul(
-                    y_acc[h, c][:, t, :],
+                    y_acc[h, c, t0][:, t - t0, :],
                     src[:, t].rearrange("p g m -> p (g m)"),
                     ident[:],
-                    start=first and t == 0,
-                    stop=not first and t == PACK - 1,
+                    start=first and t == t0,
+                    stop=not first and t == t1 - 1,
                     is_transpose=True,
                 )
 
@@ -211,9 +213,9 @@ def tile_picked_ytgn_gru_po_kernel(
                 gg[h, c] = pair[:, c]
                 tanh_of(gg[h, c], g_acc[h, c], 1.0)
 
-        def open_result(h, c, bank):
-            y_acc[h, c] = psum.tile([P, PACK, CHUNK], F32, name=f"y_acc{h}{c}", tag=f"bank{bank}")
-            turn_add(h, c, gg[h, c], True)
+        def open_result(h, c, bank, t0=0, t1=PACK):
+            y_acc[h, c, t0] = psum.tile([P, t1 - t0, CHUNK], F32, name=f"y_acc{h}{c}{t0}", tag=f"bank{bank}")
+            turn_add(h, c, gg[h, c], True, t0, t1)
 
         def make_diff(h, c, tag):
             diff[h, c] = sb.tile([P, PACK, 2, WORDS], F32, name=f"diff{h}{c}", tag=tag, align_bytes=64)
@@ -227,43 +229,42 @@ def tile_picked_ytgn_gru_po_kernel(
                     op1=ADD,
                 )
 
-        def gate_tanh(h, c):
+        def gate_tanh(h, c, parts):
             products(z_acc, "r1", h, c, False)
-            tanh_of(th[h, c][:], z_acc[h, c], 0.5)
+            for t0, t1 in parts:
+                tanh_of(th[h, c][:], z_acc[h, c], 0.5, t0, t1)
 
-        def gate(h, c, tag):
-            gated[h, c] = sb.tile([P, PACK, 2, WORDS], F32, name=f"gated{h}{c}", tag=tag, align_bytes=64)
+        def gate(h, c, t0=0, t1=PACK):
             nc.vector.scalar_tensor_tensor(
-                out=gated[h, c][:].rearrange("p t g m -> p (t g m)"),
-                in0=th[h, c][:].rearrange("p t g m -> p (t g m)"),
+                out=gated[h, c][:, t0:t1].rearrange("p t g m -> p (t g m)"),
+                in0=th[h, c][:, t0:t1].rearrange("p t g m -> p (t g m)"),
                 scalar=1.0,
-                in1=diff[h, c][:].rearrange("p t g m -> p (t g m)"),
+                in1=diff[h, c][:, t0:t1].rearrange("p t g m -> p (t g m)"),
                 op0=SUB,
                 op1=MULT,
             )
-            turn_add(h, c, gated[h, c], False)
+            turn_add(h, c, gated[h, c], False, t0, t1)
 
-        def take_out(engine, h, c):
-            copy_on(engine, y[h][:, :, c, :], y_acc[h, c][:])
+        def take_out(engine, h, c, t0=0, t1=PACK):
+            copy_on(engine, y[h][:, t0:t1, c, :], y_acc[h, c, t0][:])
 
-        def store_rows(h):
-            for g, queue in enumerate((nc.sync, nc.scalar)):
+        def store_rows(h, queues):
+            for g, queue in enumerate(queues):
                 queue.dma_start(out_rows[h, g], y[h][g * WORDS : (g + 1) * WORDS].rearrange("p t c j -> p t (c j)"))
 
-        def round_out(engine, h, c):
-            interleave(engine, y_bf[h, c][:], y[h][:, :, c, :])
+        def round_out(engine, dst, h, c):
+            interleave(engine, dst, y[h][:, :, c, :])
 
-        def quantize_out(h, c):
-            cols = slice(c * CHUNK, (c + 1) * CHUNK)
+        def quantize_out(src, h, cols):
             nc.vector.quantize_mx(
                 out=y_codes[:, h, cols].bitcast(FP8X4),
                 scales=y_scales[4 * h :, cols],
-                in_=y_bf[h, c][:].rearrange("p s t -> p (s t)"),
+                in_=src.rearrange("p s t -> p (s t)"),
             )
 
-        def store_words(h, queues):
-            for g, queue in enumerate(queues):
-                queue.dma_start(out_words[g][:, h, :], y_codes[g * WORDS : (g + 1) * WORDS, h, :])
+        def store_words():
+            for g, queue in enumerate((nc.sync, nc.scalar)):
+                queue.dma_start(out_words[g], y_codes[g * WORDS : (g + 1) * WORDS])
 
         def store_scales():
             for q in range(4):
@@ -289,6 +290,8 @@ def tile_picked_ytgn_gru_po_kernel(
             load_weight(n, h)
 
         both = range(2)
+        whole = [(0, PACK)]
+        pairs = [(0, 2), (2, PACK)]
         gather_mem("scalar", 0)
         gather_x_scales()
         gather_mem("vector", 1)
@@ -320,7 +323,7 @@ def tile_picked_ytgn_gru_po_kernel(
         prepare("scalar", "r2", 1)
         prepare("vector", "w2", 1)
         for c in both:
-            gate_tanh(0, c)
+            gate_tanh(0, c, whole)
         for c in both:
             open_sum(g_acc, "g_acc", "r2", 1, c, 6 + c)
             products(g_acc, "w2", 1, c, False)
@@ -329,7 +332,7 @@ def tile_picked_ytgn_gru_po_kernel(
         prepare("vector", "r1", 1)
         for c in both:
             open_sum(z_acc, "z_acc", "w1", 1, c, 6 + c)
-            gate_tanh(1, c)
+            gate_tanh(1, c, pairs)
         for c in both:
             for g in both:
                 turn_ov(g, c)
@@ -338,18 +341,27 @@ def tile_picked_ytgn_gru_po_kernel(
             open_result(0, c, 4 + c)
         for c in both:
             make_diff(1, c, f"diff1{c}")
-            open_result(1, c, 2 * c)
-        gate(0, 0, "gated00")
-        gate(0, 1, "gated01")
-        gate(1, 0, "gated10")
-        gate(1, 1, "gated11")
-        for h in both:
-            for c in both:
-                take_out("scalar", h, c)
-            store_rows(h)
-        for h in both:
-            for c in both:
-                round_out("vector", h, c)
-                quantize_out(h, c)
-            store_words(h, (nc.sync, nc.scalar if h else nc.sync))
+            for t0, t1 in pairs:
+                open_result(1, c, 2 * c + t0 // 2, t0, t1)
+        for c in both:
+            gate(0, c)
+        for c in both:
+            for t0, t1 in pairs:
+                gate(1, c, t0, t1)
+        for c in both:
+            take_out("scalar", 0, c)
+        store_rows(0, (nc.sync, nc.sync))
+        for c in both:
+            for t0, t1 in pairs:
+                take_out("scalar", 1, c, t0, t1)
+        store_rows(1, (nc.sync, nc.scalar))
+        for c, tag in enumerate(("y_bf00", "th11")):
+            rounded = sb.tile([P, CHUNK, PACK], BF16, name=f"y_bf0{c}", tag=tag, align_bytes=64)
+            round_out("vector", rounded[:], 0, c)
+            quantize_out(rounded[:], 0, slice(c * CHUNK, (c + 1) * CHUNK))
+        rounded = sb.tile([P, HALF, PACK], BF16, name="y_bf1", align_bytes=64)
+        for c in both:
+            round_out("vector", rounded[:, c * CHUNK : (c + 1) * CHUNK, :], 1, c)
+        quantize_out(rounded[:], 1, slice(0, HALF))
+        store_words()
         store_scales()

@@ -90,7 +90,7 @@ def tile_picked_ytgn_gru_po_kernel(
 
         def load_scales(queue, q):
             queue.dma_start(
-                xs_all[32 * q : 32 * q + 4, :].bitcast(I32), x_scales[0, 4 * q : 4 * q + 4, :].bitcast(I32)
+                xs_all[q:P:32, :].bitcast(I32), x_scales[0, q:16:4, :].bitcast(I32)
             )
 
         def load_mem(t):
@@ -331,26 +331,26 @@ def tile_picked_ytgn_gru_po_kernel(
         prepare("scalar", "w1", 1)
         prepare("vector", "r1", 1)
         for c in both:
-            open_sum(z_acc, "z_acc", "w1", 1, c, 6 + c)
-            gate_tanh(1, c, pairs)
-        for c in both:
             for g in both:
                 turn_ov(g, c)
         for c in both:
             make_diff(0, c, f"diff0{c}")
             open_result(0, c, 4 + c)
         for c in both:
+            gate(0, c)
+        for c in both:
+            take_out("scalar", 0, c)
+        store_rows(0, (nc.sync, nc.scalar))
+        for c in both:
+            open_sum(z_acc, "z_acc", "w1", 1, c, 6 + c)
+            gate_tanh(1, c, pairs)
+        for c in both:
             make_diff(1, c, f"diff1{c}")
             for t0, t1 in pairs:
                 open_result(1, c, 2 * c + t0 // 2, t0, t1)
         for c in both:
-            gate(0, c)
-        for c in both:
             for t0, t1 in pairs:
                 gate(1, c, t0, t1)
-        for c in both:
-            take_out("scalar", 0, c)
-        store_rows(0, (nc.sync, nc.sync))
         for c in both:
             for t0, t1 in pairs:
                 take_out("scalar", 1, c, t0, t1)

@@ -104,7 +104,7 @@ def tile_picked_ytgn_gru_po_kernel(
             nc.sync.dma_start(xw_all[:], x_words[0].rearrange("p n t -> p (n t)").bitcast(I32))
 
         def load_unit():
-            nc.sync.dma_start(unit_t[:], unit.rearrange("(p t) o -> p (t o)", t=PACK))
+            nc.gpsimd.dma_start(unit_t[:], unit.rearrange("(p t) o -> p (t o)", t=PACK))
 
         def gather_mem(engine, t, a=0, b=S):
             window = mem_t[t][:].indirect(slot_t[:, a // 16 : b // 16])
@@ -248,9 +248,12 @@ def tile_picked_ytgn_gru_po_kernel(
         def take_out(engine, h, c, t0=0, t1=PACK):
             copy_on(engine, y[h][:, t0:t1, c, :], y_acc[h, c, t0][:])
 
-        def store_rows(h, queues):
-            for g, queue in enumerate(queues):
-                queue.dma_start(out_rows[h, g], y[h][g * WORDS : (g + 1) * WORDS].rearrange("p t c j -> p t (c j)"))
+        def store_rows(h, c0, c1):
+            for g, queue in enumerate((nc.sync, nc.scalar)):
+                queue.dma_start(
+                    out_rows[h, g][:, :, c0 * CHUNK : c1 * CHUNK],
+                    y[h][g * WORDS : (g + 1) * WORDS, :, c0:c1, :].rearrange("p t c j -> p t (c j)"),
+                )
 
         def round_out(engine, dst, h, c):
             interleave(engine, dst, y[h][:, :, c, :])
@@ -274,15 +277,15 @@ def tile_picked_ytgn_gru_po_kernel(
         nc.vector.memset(xs_all[:].bitcast(I32), 0)
         nc.vector.memset(zero_in[:], 0.0)
         nc.scalar.activation(out=zero[:], in_=zero_in[:], func=TANH)
+        load_unit()
         make_identity(nc, ident[:])
-        nc.sync.dma_start(slot_t[:], slot)
-        nc.sync.dma_start(offs_t[:], offs)
         load_mem(0)
+        nc.sync.dma_start(slot_t[:], slot)
+        load_mem(1)
+        load_mem(2)
+        nc.sync.dma_start(offs_t[:], offs)
         for q in range(4):
             load_scales(nc.sync, q)
-        load_mem(1)
-        load_unit()
-        load_mem(2)
         load_mem(3)
         load_weight("r2", 0)
         load_x()
@@ -340,7 +343,7 @@ def tile_picked_ytgn_gru_po_kernel(
             gate(0, c)
         for c in both:
             take_out("scalar", 0, c)
-        store_rows(0, (nc.sync, nc.scalar))
+        store_rows(0, 0, 2)
         for c in both:
             open_sum(z_acc, "z_acc", "w1", 1, c, 6 + c)
             gate_tanh(1, c, pairs)
@@ -354,8 +357,8 @@ def tile_picked_ytgn_gru_po_kernel(
         for c in both:
             for t0, t1 in pairs:
                 take_out("scalar", 1, c, t0, t1)
-        store_rows(1, (nc.sync, nc.scalar))
-        for c, tag in enumerate(("y_bf00", "th11")):
+            store_rows(1, c, c + 1)
+        for c, tag in enumerate(("y_bf00", "th10")):
             rounded = sb.tile([P, CHUNK, PACK], BF16, name=f"y_bf0{c}", tag=tag, align_bytes=64)
             round_out("vector", rounded[:], 0, c)
             quantize_out(rounded[:], 0, slice(c * CHUNK, (c + 1) * CHUNK))

@@ -104,7 +104,7 @@ def tile_picked_ytgn_gru_po_kernel(
             nc.sync.dma_start(xw_all[:], x_words[0].rearrange("p n t -> p (n t)").bitcast(I32))
 
         def load_unit():
-            nc.gpsimd.dma_start(unit_t[:], unit.rearrange("(p t) o -> p (t o)", t=PACK))
+            nc.sync.dma_start(unit_t[:], unit.rearrange("(p t) o -> p (t o)", t=PACK))
 
         def gather_mem(engine, t, a=0, b=S):
             window = mem_t[t][:].indirect(slot_t[:, a // 16 : b // 16])
@@ -277,15 +277,15 @@ def tile_picked_ytgn_gru_po_kernel(
         nc.vector.memset(xs_all[:].bitcast(I32), 0)
         nc.vector.memset(zero_in[:], 0.0)
         nc.scalar.activation(out=zero[:], in_=zero_in[:], func=TANH)
-        load_unit()
         make_identity(nc, ident[:])
-        load_mem(0)
         nc.sync.dma_start(slot_t[:], slot)
-        load_mem(1)
-        load_mem(2)
         nc.sync.dma_start(offs_t[:], offs)
+        load_mem(0)
         for q in range(4):
             load_scales(nc.sync, q)
+        load_mem(1)
+        load_unit()
+        load_mem(2)
         load_mem(3)
         load_weight("r2", 0)
         load_x()

@@ -75,7 +75,6 @@ def tile_picked_ytgn_gru_po_kernel(
         diff = {}
         gated = {b: sb.tile([P, PACK, 2, WORDS], F32, name=f"gated{b[0]}{b[1]}") for b in blocks}
         y = [sb.tile([P, PACK, 2, CHUNK], F32, name=f"y{h}") for h in range(2)]
-        y_codes = sb.tile([P, 2, HALF], I32, name="y_codes", align_bytes=64)
         y_scales = sb.tile([P, HALF], U8, name="y_scales", align_bytes=64)
         out_rows = out_0.rearrange("(h m t) (g j) -> h g m t j", h=2, t=PACK, g=2)
         out_words = out_1[0].rearrange("p c r -> p (c r)").bitcast(I32).rearrange("(h m) (g j) -> g m h j", h=2, g=2)
@@ -135,8 +134,8 @@ def tile_picked_ytgn_gru_po_kernel(
             for t in range(PACK):
                 nc.tensor.transpose(bank[:, t, :], ov[t][:, cols_of(g, c)], ident[:])
 
-        def round_weight(engine, n, h):
-            interleave(engine, w_bf[n, h][:], raw[n, h][:])
+        def round_weight(engine, n, h, a=0, b=HALF):
+            interleave(engine, w_bf[n, h][:, a:b, :], raw[n, h][:, :, a:b])
 
         def prepare(engine, n, h):
             round_weight(engine, n, h)
@@ -331,7 +330,9 @@ def tile_picked_ytgn_gru_po_kernel(
             open_sum(g_acc, "g_acc", "r2", 1, c, 6 + c)
             products(g_acc, "w2", 1, c, False)
         candidate(1, "gg1")
-        prepare("scalar", "w1", 1)
+        round_weight("scalar", "w1", 1, 0, 192)
+        round_weight("vector", "w1", 1, 192, HALF)
+        quantize_weight("w1", 1)
         prepare("vector", "r1", 1)
         for c in both:
             for g in both:
@@ -358,13 +359,11 @@ def tile_picked_ytgn_gru_po_kernel(
             for t0, t1 in pairs:
                 take_out("scalar", 1, c, t0, t1)
             store_rows(1, c, c + 1)
-        for c, tag in enumerate(("y_bf00", "th10")):
-            rounded = sb.tile([P, CHUNK, PACK], BF16, name=f"y_bf0{c}", tag=tag, align_bytes=64)
-            round_out("vector", rounded[:], 0, c)
-            quantize_out(rounded[:], 0, slice(c * CHUNK, (c + 1) * CHUNK))
-        rounded = sb.tile([P, HALF, PACK], BF16, name="y_bf1", align_bytes=64)
-        for c in both:
-            round_out("vector", rounded[:, c * CHUNK : (c + 1) * CHUNK, :], 1, c)
-        quantize_out(rounded[:], 1, slice(0, HALF))
+        y_codes = sb.tile([P, 2, HALF], I32, name="y_codes", tag="th11", align_bytes=64)
+        for h in both:
+            rounded = sb.tile([P, HALF, PACK], BF16, name=f"y_bf{h}", align_bytes=64)
+            for c in both:
+                round_out("vector", rounded[:, c * CHUNK : (c + 1) * CHUNK, :], h, c)
+            quantize_out(rounded[:], h, slice(0, HALF))
         store_words()
         store_scales()

@@ -24,6 +24,7 @@ PACK = 4
 HALF = 256
 CHUNK = 128
 WORDS = HALF // PACK
+WARM_UPS = 3
 
 
 def tile_picked_ytgn_gru_po_kernel(
@@ -307,6 +308,17 @@ def tile_picked_ytgn_gru_po_kernel(
             round_old("vector", c)
         for c in both:
             quantize_old(c)
+        warm = psum.tile([P, 2, HALF], F32, name="warm", tag="bank6")
+        for i in range(WARM_UPS):
+            nc.tensor.matmul_mx(
+                out=warm[:, 0, :],
+                lhsT=old_codes[0][:, 0, :].bitcast(FP8X4),
+                lhsT_scale=old_scales[0][:, 0, :],
+                rhs=old_codes[0][:].rearrange("p g j -> p (g j)").bitcast(FP8X4),
+                rhs_scale=old_scales[0][:].rearrange("p g j -> p (g j)"),
+                start=i == 0,
+                stop=i == WARM_UPS - 1,
+            )
         prepare("scalar", "r2", 0)
         for c in both:
             open_sum(g_acc, "g_acc", "r2", 0, c, 4 + c)

@@ -354,8 +354,8 @@ def tile_picked_ytgn_gru_po_kernel(
             open_result(0, c, 4 + c)
         for c in both:
             gate(0, c)
-        for c in both:
-            take_out("scalar", 0, c)
+        for c, engine in enumerate(("scalar", "vector")):
+            take_out(engine, 0, c)
         store_rows(0, 0, 2)
         for c in both:
             open_sum(z_acc, "z_acc", "w1", 1, c, 6 + c)
@@ -371,9 +371,9 @@ def tile_picked_ytgn_gru_po_kernel(
             for t0, t1 in pairs:
                 take_out("scalar", 1, c, t0, t1)
             store_rows(1, c, c + 1)
-        y_codes = sb.tile([P, 2, HALF], I32, name="y_codes", tag="th11", align_bytes=64)
-        for h in both:
-            rounded = sb.tile([P, HALF, PACK], BF16, name=f"y_bf{h}", align_bytes=64)
+        y_codes = sb.tile([P, 2, HALF], I32, name="y_codes", align_bytes=64)
+        for h, tag in enumerate(("th11", "y_bf1")):
+            rounded = sb.tile([P, HALF, PACK], BF16, name=f"y_bf{h}", tag=tag, align_bytes=64)
             for c in both:
                 round_out("vector", rounded[:, c * CHUNK : (c + 1) * CHUNK, :], h, c)
             quantize_out(rounded[:], h, slice(0, HALF))

@@ -24,7 +24,6 @@ PACK = 4
 HALF = 256
 CHUNK = 128
 WORDS = HALF // PACK
-WARM_UPS = 3
 
 
 def tile_picked_ytgn_gru_po_kernel(
@@ -308,17 +307,6 @@ def tile_picked_ytgn_gru_po_kernel(
             round_old("vector", c)
         for c in both:
             quantize_old(c)
-        warm = psum.tile([P, 2, HALF], F32, name="warm", tag="bank6")
-        for i in range(WARM_UPS):
-            nc.tensor.matmul_mx(
-                out=warm[:, 0, :],
-                lhsT=old_codes[0][:, 0, :].bitcast(FP8X4),
-                lhsT_scale=old_scales[0][:, 0, :],
-                rhs=old_codes[0][:].rearrange("p g j -> p (g j)").bitcast(FP8X4),
-                rhs_scale=old_scales[0][:].rearrange("p g j -> p (g j)"),
-                start=i == 0,
-                stop=i == WARM_UPS - 1,
-            )
         prepare("scalar", "r2", 0)
         for c in both:
             open_sum(g_acc, "g_acc", "r2", 0, c, 4 + c)

from contextlib import ExitStack

import concourse.mybir as mybir
from concourse.masks import make_identity

K, T, S, H, U = 512, 1024, 512, 512, 1024
FLOPS = 4 * 2 * K * H * S

F32 = mybir.dt.float32
BF16 = mybir.dt.bfloat16
I32 = mybir.dt.int32
U32 = mybir.dt.uint32
U16 = mybir.dt.uint16
U8 = mybir.dt.uint8
FP8X4 = mybir.dt.float8_e4m3fn_x4
TANH = mybir.ActivationFunctionType.Tanh
COPY = mybir.ActivationFunctionType.Copy
MULT = mybir.AluOpType.mult
ADD = mybir.AluOpType.add
SUB = mybir.AluOpType.subtract

P = 128
PACK = 4
HALF = 256
CHUNK = 128
WORDS = HALF // PACK


def tile_picked_ytgn_gru_po_kernel(
    tc, x_words, x_scales, mem, w1, w2, r1, r2, unit, offs, slot, out_0, out_1, out_2
):
    nc = tc.nc
    with ExitStack() as ctx:
        sb = ctx.enter_context(tc.tile_pool(name="sb", bufs=1))
        psum = ctx.enter_context(tc.psum_pool(name="psum", bufs=1))

        def copy_on(engine, out, in_):
            if engine == "scalar":
                nc.scalar.copy(out=out, in_=in_)
            else:
                nc.vector.tensor_copy(out=out, in_=in_)

        slot_t = sb.tile([P, S // 16], U16, name="slot_t")
        offs_t = sb.tile([P, S // 16], U16, name="offs_t")
        xs_all = sb.tile([P, T], U8, name="xs_all", align_bytes=64)
        xw_all = sb.tile([P, T], I32, name="xw_all", align_bytes=64)
        unit_t = sb.tile([P, PACK], F32, name="unit_t")
        zero_in = sb.tile([P, 1], F32, name="zero_in")
        zero = sb.tile([P, 1], F32, name="zero")
        ident = sb.tile([P, P], F32, name="ident")
        mem_rows = mem.rearrange("(p t) c -> p t c", t=PACK)
        mem_t = [sb.tile([P, U], F32, name=f"mem{t}", tag=f"mem{t}") for t in range(PACK)]
        weights = {"w1": w1, "w2": w2, "r1": r1, "r2": r2}
        pieces = [(n, h) for n in weights for h in range(2)]
        raw = {k: sb.tile([P, PACK, HALF], F32, name=f"raw_{k[0]}_{k[1]}", tag=f"raw_{k[0]}_{k[1]}") for k in pieces}
        w_bf = {
            k: sb.tile([P, HALF, PACK], BF16, name=f"bf_{k[0]}_{k[1]}", tag=f"bf_{k[0]}_{k[1]}", align_bytes=64)
            for k in pieces
        }
        w_codes = {k: sb.tile([P, HALF], U32, name=f"codes_{k[0]}_{k[1]}", align_bytes=64) for k in pieces}
        w_scales = {k: sb.tile([P, HALF], U8, name=f"scales_{k[0]}_{k[1]}", align_bytes=64) for k in pieces}
        old = sb.tile([P, PACK, S], F32, name="old")
        ov = {}
        unit_half = sb.tile([P, PACK], F32, name="unit_half")
        old_bf = [sb.tile([P, 2, CHUNK, PACK], BF16, name=f"old_bf{c}", align_bytes=64) for c in range(2)]
        old_codes = [sb.tile([P, 2, CHUNK], U32, name=f"old_codes{c}", align_bytes=64) for c in range(2)]
        old_scales = [sb.tile([P, 2, CHUNK], U8, name=f"old_scales{c}", align_bytes=64) for c in range(2)]
        x_sc = sb.tile([P, S], U8, name="x_sc", align_bytes=64)
        blocks = [(h, c) for h in range(2) for c in range(2)]
        gg = {}
        th = {
            b: sb.tile([P, PACK, 2, WORDS], F32, name=f"th{b[0]}{b[1]}", tag=f"th{b[0]}{b[1]}", align_bytes=64)
            for b in blocks
        }
        diff = {}
        gated = {b: sb.tile([P, PACK, 2, WORDS], F32, name=f"gated{b[0]}{b[1]}") for b in blocks}
        y = [sb.tile([P, PACK, 2, CHUNK], F32, name=f"y{h}") for h in range(2)]
        y_scales = sb.tile([P, HALF], U8, name="y_scales", align_bytes=64)
        out_rows = out_0.rearrange("(h m t) (g j) -> h g m t j", h=2, t=PACK, g=2)
        out_words = out_1[0].rearrange("p c r -> p (c r)").bitcast(I32).rearrange("(h m) (g j) -> g m h j", h=2, g=2)
        out_scales = out_2[0].bitcast(I32).rearrange("(h a r) (g c) -> a g h r c", h=2, a=2, g=2)
        ov_turned = {}
        g_acc = {}
        z_acc = {}
        y_acc = {}

        def cols_of(g, c):
            return slice(g * HALF + c * CHUNK, g * HALF + (c + 1) * CHUNK)

        def load_scales(queue, q):
            queue.dma_start(
                xs_all[q:P:32, :].bitcast(I32), x_scales[0, q:16:4, :].bitcast(I32)
            )

        def load_mem(t):
            nc.sync.dma_start(mem_t[t][:], mem_rows[:, t, :])

        def load_weight(n, h):
            rows = weights[n].rearrange("(p j) c -> p j c", j=PACK)
            nc.sync.dma_start(raw[n, h][:], rows[:, :, h * HALF : (h + 1) * HALF])

        def load_x():
            nc.sync.dma_start(xw_all[:], x_words[0].rearrange("p n t -> p (n t)").bitcast(I32))

        def load_unit():
            nc.sync.dma_start(unit_t[:], unit.rearrange("(p t) o -> p (t o)", t=PACK))

        def gather_mem(engine, t, a=0, b=S):
            window = mem_t[t][:].indirect(slot_t[:, a // 16 : b // 16])
            if engine == "scalar":
                nc.scalar.activation(out=old[:, t, a:b], in_=window, func=COPY)
            else:
                nc.vector.tensor_copy(old[:, t, a:b], window)

        def gather_x_words():
            nc.vector.tensor_copy(x_codes[:], xw_all[:].bitcast(U32).indirect(offs_t[:]))

        def gather_x_scales():
            nc.vector.tensor_copy(x_sc[:], xs_all[:].indirect(offs_t[:]))

        def scale_old(engine, t, tag):
            ov[t] = sb.tile([P, S], F32, name=f"ov{t}", tag=tag)
            dst = ov[t][:]
            if engine == "scalar":
                nc.scalar.activation(out=dst, in_=old[:, t, :], func=COPY, scale=unit_half[:, t : t + 1])
            else:
                nc.vector.tensor_scalar(
                    out=dst, in0=old[:, t, :], scalar1=unit_half[:, t : t + 1], scalar2=None, op0=MULT
                )

        def turn_ov(g, c):
            bank = psum.tile([P, PACK, P], F32, name=f"ov_turned{g}{c}", tag=f"bank{2 * c + g}")
            ov_turned[g, c] = bank
            for t in range(PACK):
                nc.tensor.transpose(bank[:, t, :], ov[t][:, cols_of(g, c)], ident[:])

        def round_weight(engine, n, h, a=0, b=HALF):
            interleave(engine, w_bf[n, h][:, a:b, :], raw[n, h][:, :, a:b])

        def prepare(engine, n, h):
            round_weight(engine, n, h)
            quantize_weight(n, h)

        def quantize_weight(n, h):
            nc.vector.quantize_mx(
                out=w_codes[n, h][:].bitcast(FP8X4),
                scales=w_scales[n, h][:],
                in_=w_bf[n, h][:].rearrange("p c j -> p (c j)"),
            )

        def interleave(engine, dst, src):
            copy_on(
                engine,
                dst.rearrange("p (c i) t -> p c t i", i=4),
                src.rearrange("p t (c i) -> p c t i", i=4),
            )

        def round_old(engine, c):
            src = old[:].rearrange("p t (g c a i) -> p c g a t i", g=2, c=2, i=4)[:, c]
            copy_on(engine, old_bf[c][:].rearrange("p g (a i) t -> p g a t i", i=4), src)

        def quantize_old(c):
            nc.vector.quantize_mx(
                out=old_codes[c][:].rearrange("p g j -> p (g j)").bitcast(FP8X4),
                scales=old_scales[c][:].rearrange("p g j -> p (g j)"),
                in_=old_bf[c][:].rearrange("p g j t -> p (g j t)"),
            )

        def products(acc, n, h, c, first):
            for g in range(2):
                if n in ("w1", "w2"):
                    codes, scales = x_codes[:, cols_of(g, c)], x_sc[:, cols_of(g, c)]
                else:
                    codes, scales = old_codes[c][:, g, :], old_scales[c][:, g, :]
                nc.tensor.matmul_mx(
                    out=acc[h, c][:, g, :],
                    lhsT=codes.bitcast(FP8X4),
                    lhsT_scale=scales,
                    rhs=w_codes[n, h][:].bitcast(FP8X4),
                    rhs_scale=w_scales[n, h][:],
                    start=first and g == 0,
                    stop=not first and g == 1,
                )

        def open_sum(acc, name, n, h, c, bank):
            acc[h, c] = psum.tile([P, 2, HALF], F32, name=f"{name}{h}{c}", tag=f"bank{bank}")
            products(acc, n, h, c, True)

        def tanh_of(dst, acc, scale, t0=0, t1=PACK):
            nc.scalar.activation(
                out=dst[:, t0:t1].rearrange("p t g m -> p t (g m)"),
                in_=acc[:].rearrange("p g (m t) -> p t (g m)", t=PACK)[:, t0:t1],
                func=TANH,
                bias=zero[:],
                scale=scale,
            )

        def turn_add(h, c, src, first, t0, t1):
            for t in range(t0, t1):
                nc.tensor.matmul(
                    y_acc[h, c, t0][:, t - t0, :],
                    src[:, t].rearrange("p g m -> p (g m)"),
                    ident[:],
                    start=first and t == t0,
                    stop=not first and t == t1 - 1,
                    is_transpose=True,
                )

        def candidate(h, tag):
            pair = sb.tile([P, 2, PACK, 2, WORDS], F32, name=f"gg{h}", tag=tag)
            for c in range(2):
                gg[h, c] = pair[:, c]
                tanh_of(gg[h, c], g_acc[h, c], 1.0)

        def open_result(h, c, bank, t0=0, t1=PACK):
            y_acc[h, c, t0] = psum.tile([P, t1 - t0, CHUNK], F32, name=f"y_acc{h}{c}{t0}", tag=f"bank{bank}")
            turn_add(h, c, gg[h, c], True, t0, t1)

        def make_diff(h, c, tag):
            diff[h, c] = sb.tile([P, PACK, 2, WORDS], F32, name=f"diff{h}{c}", tag=tag, align_bytes=64)
            for g in range(2):
                nc.vector.scalar_tensor_tensor(
                    out=diff[h, c][:, :, g, :],
                    in0=gg[h, c][:, :, g, :],
                    scalar=0.5,
                    in1=ov_turned[g, c][:, :, h * WORDS : (h + 1) * WORDS],
                    op0=MULT,
                    op1=ADD,
                )

        def gate_tanh(h, c, parts):
            products(z_acc, "r1", h, c, False)
            for t0, t1 in parts:
                tanh_of(th[h, c][:], z_acc[h, c], 0.5, t0, t1)

        def gate(h, c, t0=0, t1=PACK):
            nc.vector.scalar_tensor_tensor(
                out=gated[h, c][:, t0:t1].rearrange("p t g m -> p (t g m)"),
                in0=th[h, c][:, t0:t1].rearrange("p t g m -> p (t g m)"),
                scalar=1.0,
                in1=diff[h, c][:, t0:t1].rearrange("p t g m -> p (t g m)"),
                op0=SUB,
                op1=MULT,
            )
            turn_add(h, c, gated[h, c], False, t0, t1)

        def take_out(engine, h, c, t0=0, t1=PACK):
            copy_on(engine, y[h][:, t0:t1, c, :], y_acc[h, c, t0][:])

        def store_rows(h, c0, c1):
            for g, queue in enumerate((nc.sync, nc.scalar)):
                queue.dma_start(
                    out_rows[h, g][:, :, c0 * CHUNK : c1 * CHUNK],
                    y[h][g * WORDS : (g + 1) * WORDS, :, c0:c1, :].rearrange("p t c j -> p t (c j)"),
                )

        def round_out(engine, dst, h, c):
            interleave(engine, dst, y[h][:, :, c, :])

        def quantize_out(src, h, cols):
            nc.vector.quantize_mx(
                out=y_codes[:, h, cols].bitcast(FP8X4),
                scales=y_scales[4 * h :, cols],
                in_=src.rearrange("p s t -> p (s t)"),
            )

        def store_words():
            for g, queue in enumerate((nc.sync, nc.scalar)):
                queue.dma_start(out_words[g], y_codes[g * WORDS : (g + 1) * WORDS])

        def store_scales():
            for q in range(4):
                queue = nc.sync if q % 2 else nc.scalar
                queue.dma_start(out_scales[q % 2, q // 2], y_scales[32 * q : 32 * q + 8, :].bitcast(I32))

        nc.vector.memset(xs_all[:].bitcast(I32), 0)
        nc.vector.memset(zero_in[:], 0.0)
        nc.scalar.activation(out=zero[:], in_=zero_in[:], func=TANH)
        make_identity(nc, ident[:])
        nc.sync.dma_start(slot_t[:], slot)
        nc.sync.dma_start(offs_t[:], offs)
        load_mem(0)
        for q in range(4):
            load_scales(nc.sync, q)
        load_mem(1)
        load_unit()
        load_mem(2)
        load_mem(3)
        load_weight("r2", 0)
        load_x()
        for n, h in (("w2", 0), ("w1", 0), ("r1", 0), ("r2", 1), ("w2", 1), ("w1", 1), ("r1", 1)):
            load_weight(n, h)

        both = range(2)
        whole = [(0, PACK)]
        pairs = [(0, 2), (2, PACK)]
        gather_mem("scalar", 0)
        gather_x_scales()
        gather_mem("vector", 1)
        gather_mem("scalar", 2)
        gather_mem("vector", 3, 0, HALF)
        gather_mem("scalar", 3, HALF, S)
        nc.gpsimd.tensor_scalar(out=unit_half[:], in0=unit_t[:], scalar1=-0.5, scalar2=0.0, op0=MULT, op1=ADD)
        scale_old("scalar", 0, "ov0")
        scale_old("vector", 1, "ov1")
        for c in both:
            round_old("vector", c)
        for c in both:
            quantize_old(c)
        prepare("scalar", "r2", 0)
        for c in both:
            open_sum(g_acc, "g_acc", "r2", 0, c, 4 + c)
        x_codes = sb.tile([P, S], U32, name="x_codes", tag="bf_r2_0", align_bytes=64)
        gather_x_words()
        scale_old("scalar", 2, "mem3")
        scale_old("vector", 3, "ov3")
        prepare("scalar", "w2", 0)
        for c in both:
            products(g_acc, "w2", 0, c, False)
        candidate(0, "gg0")
        prepare("scalar", "w1", 0)
        prepare("vector", "r1", 0)
        for c in both:
            open_sum(z_acc, "z_acc", "w1", 0, c, 6 + c)
        prepare("scalar", "r2", 1)
        prepare("vector", "w2", 1)
        for c in both:
            gate_tanh(0, c, whole)
        for c in both:
            open_sum(g_acc, "g_acc", "r2", 1, c, 6 + c)
            products(g_acc, "w2", 1, c, False)
        candidate(1, "gg1")
        round_weight("scalar", "w1", 1, 0, 192)
        round_weight("vector", "w1", 1, 192, HALF)
        quantize_weight("w1", 1)
        prepare("vector", "r1", 1)
        for c in both:
            for g in both:
                turn_ov(g, c)
        for c in both:
            make_diff(0, c, f"diff0{c}")
            open_result(0, c, 4 + c)
        for c in both:
            gate(0, c)
        for c, engine in enumerate(("scalar", "vector")):
            take_out(engine, 0, c)
        store_rows(0, 0, 2)
        for c in both:
            open_sum(z_acc, "z_acc", "w1", 1, c, 6 + c)
            gate_tanh(1, c, pairs)
        for c in both:
            make_diff(1, c, f"diff1{c}")
            for t0, t1 in pairs:
                open_result(1, c, 2 * c + t0 // 2, t0, t1)
        for c in both:
            for t0, t1 in pairs:
                gate(1, c, t0, t1)
        for c in both:
            for t0, t1 in pairs:
                take_out("scalar", 1, c, t0, t1)
            store_rows(1, c, c + 1)
        y_codes = sb.tile([P, 2, HALF], I32, name="y_codes", align_bytes=64)
        for h, tag in enumerate(("th11", "y_bf1")):
            rounded = sb.tile([P, HALF, PACK], BF16, name=f"y_bf{h}", tag=tag, align_bytes=64)
            for c in both:
                round_out("vector", rounded[:, c * CHUNK : (c + 1) * CHUNK, :], h, c)
            quantize_out(rounded[:], h, slice(0, HALF))
        store_words()
        store_scales()
